import numpy as np
import ml_dtypes


def mxq(x, axis, fmt="e4m3"):
    dtype, down = {"e4m3": (ml_dtypes.float8_e4m3fn, 7), "e5m2": (ml_dtypes.float8_e5m2, 14)}[fmt]
    v = np.moveaxis(np.asarray(x, np.float32).astype(ml_dtypes.bfloat16).astype(np.float64), axis, -1)
    blocks = v.reshape(v.shape[:-1] + (-1, 32))
    amax = np.abs(blocks).max(-1, keepdims=True)
    byte = np.maximum(np.where(amax > 0, np.frexp(amax)[1] - 1 + 127, 0) - down, 1)
    scale = np.exp2(byte - 127.0)
    codes = (blocks / scale).astype(np.float32).astype(dtype).astype(np.float64)
    return np.moveaxis((codes * scale).reshape(v.shape), -1, axis)


WIDE = False


def mx_kscale(k):
    if not WIDE:
        return np.ones(k)
    levels = np.array([18, -18])
    if k % 512:
        return np.exp2(np.random.permutation(np.resize(levels, k // 32))).repeat(32)
    a = np.empty((k // 512, 16))
    for p in range(k // 512):
        a[p, :8] = np.random.permutation(np.resize(levels, 8))
        for g in range(8):
            far = levels[np.abs(levels - a[p, g]) >= 10]
            a[p, g + 8] = far[np.random.randint(len(far))]
    return np.exp2(a.ravel()).repeat(32)


def f64(x):
    return np.asarray(x).astype(np.float64)


def striped(idx):
    return np.tile(np.asarray(idx).reshape(-1, 16).T, (8, 1)).astype(np.uint16)


def unstriped(offs):
    return offs[:16].T.reshape(-1).astype(np.int64)


def setup_inputs():
    n = np.random.standard_normal
    uni = np.random.uniform
    uidx = np.random.permutation(2048)[:512]
    idx = np.random.permutation(2048)[:512]
    f_i = np.ones(2048)
    f_i[idx] = mx_kscale(512)
    f_r = np.ones(2048)
    f_r[uidx] = mx_kscale(512)
    return {
        "G": (n((512, 512)) / np.sqrt(512) * f_i[idx][None, :]).astype(np.float32),
        "uT": (n((512, 2048)) * f_r[None, :]).astype(np.float32),
        "vT": (n((512, 2048)) / f_i[None, :]).astype(np.float32),
        "su": np.tile(uni(0.75, 1.3, 2048) / f_r, (128, 1)).astype(np.float32),
        "uoffs": striped(uidx),
        "offs": striped(idx),
    }


def reference(G, uT, vT, su, uoffs, offs):
    uidx = unstriped(uoffs)
    idx = unstriped(offs)
    uT_r = f64(uT)[:, uidx]
    vT_i = f64(vT)[:, idx]
    su_r = f64(su)[:1][:, uidx]
    c = mxq(vT_i, 1, "e4m3") @ mxq(f64(G), 1, "e5m2").T
    dc = su_r * c
    out = mxq(uT_r, 1, "e4m3") @ mxq(dc, 1, "e5m2").T
    return out

@@ -1,0 +1,136 @@
+from contextlib import ExitStack
+
+import concourse.mybir as mybir
+from concourse.masks import make_identity
+
+F32 = mybir.dt.float32
+BF16 = mybir.dt.bfloat16
+U32 = mybir.dt.uint32
+U16 = mybir.dt.uint16
+U8 = mybir.dt.uint8
+E4M3 = mybir.dt.float8_e4m3fn_x4
+E5M2 = mybir.dt.float8_e5m2_x4
+
+P = 128
+SLOTS = 512
+TABLE = 2048
+BLOCKS = 4
+
+FLOPS = 2 * 2 * 512 * 512 * 512
+BYTES = 4 * (2 * 512 * 2048 + 2 * 512 * 512 + 2048) + 2 * 2 * 128 * 32
+
+
+def tile_attend_gbil_R_kernel(tc, G, uT, vT, su, uoffs, offs, out):
+    nc = tc.nc
+    with ExitStack() as ctx:
+        keep = ctx.enter_context(tc.tile_pool(name="keep", bufs=1))
+        turn = ctx.enter_context(tc.psum_pool(name="turn", bufs=4))
+        sums = ctx.enter_context(tc.psum_pool(name="sums", bufs=4))
+
+        su_first = keep.tile([1, TABLE], F32, name="su_first")
+        nc.sync.dma_start(out=su_first[:], in_=su[0:1, :])
+        g_rows = keep.tile([P, 4 * SLOTS], F32, name="g_rows")
+        nc.sync.dma_start(out=g_rows[:], in_=G.rearrange("(m j) i -> m (j i)", j=4))
+        item_list = keep.tile([P, SLOTS // 16], U16, name="item_list")
+        nc.sync.dma_start(item_list[:], offs)
+        user_list = keep.tile([P, SLOTS // 16], U16, name="user_list")
+        nc.sync.dma_start(user_list[:], uoffs)
+
+        su_table = keep.tile([P, TABLE], F32, name="su_table")
+        nc.vector.memset(su_table[:], 0.0)
+        nc.vector.tensor_copy(out=su_table[0:1, :], in_=su_first[:])
+
+        v_tables, u_tables = [], []
+        for b in range(BLOCKS):
+            table = keep.tile([P, TABLE], F32, name=f"v_table{b}")
+            nc.sync.dma_start(out=table[:], in_=vT[b * P : (b + 1) * P, :])
+            v_tables.append(table)
+        for b in range(BLOCKS):
+            table = keep.tile([P, TABLE], F32, name=f"u_table{b}")
+            nc.sync.dma_start(out=table[:], in_=uT[b * P : (b + 1) * P, :])
+            u_tables.append(table)
+
+        ident = keep.tile([P, P], F32, name="ident")
+        make_identity(nc, ident[:])
+
+        su_row = keep.tile([P, SLOTS], F32, name="su_row")
+        nc.vector.tensor_copy(su_row[:], su_table[:].indirect(user_list[:]))
+        bank = turn.tile([P, 4, P], F32, name="bank")
+        for k in range(4):
+            nc.tensor.transpose(bank[:, k, :], su_row[:, k * P : (k + 1) * P], ident[:])
+        su_cols = keep.tile([P, 4], F32, name="su_cols")
+        nc.scalar.copy(out=su_cols[:], in_=bank[:, :, 0])
+        bank = turn.tile([P, 4, P], F32, name="bank")
+        for k in range(4):
+            nc.tensor.transpose(bank[:, k, :], su_cols[:, k : k + 1].to_broadcast([P, P]), ident[:])
+        su_wide = keep.tile([P, SLOTS], F32, name="su_wide")
+        nc.scalar.copy(
+            out=su_wide[:].rearrange("p (u m e) -> p u m e", u=2, e=2),
+            in_=bank[:].rearrange("p k n -> p (k n)").rearrange("p (m u e) -> p u m e", u=2, e=2),
+        )
+
+        g_bf = keep.tile([P, 4 * SLOTS], BF16, name="g_bf", align_bytes=64)
+        nc.vector.tensor_copy(out=g_bf[:], in_=g_rows[:])
+        g_words = g_bf[:].bitcast(F32)
+        g_k = keep.tile([P, 4 * SLOTS], BF16, name="g_k", align_bytes=64)
+        for h in range(2):
+            bank = turn.tile([P, 4, P], F32, name="bank")
+            for e in range(2):
+                j = 2 * h + e
+                for u in range(2):
+                    nc.tensor.transpose(bank[:, 2 * e + u, :], g_words[:, 256 * j + u : 256 * (j + 1) : 2], ident[:])
+            nc.scalar.copy(
+                out=g_k[:].bitcast(F32)[:, 512 * h : 512 * (h + 1)].rearrange("p (m x) -> p m x", x=4),
+                in_=bank[:].rearrange("p x m -> p m x"),
+            )
+        g_codes = keep.tile([P, SLOTS], U32, name="g_codes", align_bytes=64)
+        g_scales = keep.tile([P, SLOTS], U8, name="g_scales", align_bytes=64)
+        nc.vector.quantize_mx(out=g_codes[:].bitcast(E5M2), scales=g_scales[:], in_=g_k[:])
+
+        def turn_words(words0, words1, name):
+            bank = turn.tile([P, 4, P], F32, name="bank")
+            nc.tensor.transpose(bank[:, 0, :], words0, ident[:])
+            nc.tensor.transpose(bank[:, 1, :], words1, ident[:])
+            turned = keep.tile([P, 4 * P], BF16, name=name, align_bytes=64)
+            nc.scalar.copy(
+                out=turned[:].bitcast(F32).rearrange("p (n u) -> p n u", u=2),
+                in_=bank[:, 0:2, :].rearrange("p u n -> p n u"),
+            )
+            return turned
+
+        def gather_and_quantise(table, offsets, name):
+            picked = keep.tile([P, SLOTS], BF16, name=name + "_picked", align_bytes=64)
+            nc.vector.tensor_copy(picked[:], table[:].indirect(offsets[:]))
+            words = picked[:].bitcast(F32)
+            turned = turn_words(words[:, 0:256:2], words[:, 1:256:2], name + "_turned")
+            codes = keep.tile([P, P], U32, name=name + "_codes", align_bytes=64)
+            scales = keep.tile([P, P], U8, name=name + "_scales", align_bytes=64)
+            nc.vector.quantize_mx(out=codes[:].bitcast(E4M3), scales=scales[:], in_=turned[:])
+            return codes, scales
+
+        dc_codes = keep.tile([P, SLOTS], U32, name="dc_codes", align_bytes=64)
+        dc_scales = keep.tile([P, SLOTS], U8, name="dc_scales", align_bytes=64)
+        for b in range(BLOCKS):
+            codes, scales = gather_and_quantise(v_tables[b], item_list, f"v{b}")
+            acc = sums.tile([P, SLOTS], F32, name="acc")
+            nc.tensor.matmul_mx(
+                out=acc[:], lhsT=codes[:].bitcast(E4M3), lhsT_scale=scales[:],
+                rhs=g_codes[:].bitcast(E5M2), rhs_scale=g_scales[:], start=True, stop=True,
+            )
+            dc = keep.tile([P, SLOTS], BF16, name=f"dc{b}", align_bytes=64)
+            nc.vector.tensor_tensor(dc[:], acc[:], su_wide[:], mybir.AluOpType.mult)
+            words = dc[:].bitcast(F32)
+            turned = turn_words(words[:, 0:P], words[:, P : 2 * P], f"dc{b}_turned")
+            cols = slice(b * P, (b + 1) * P)
+            nc.vector.quantize_mx(out=dc_codes[:, cols].bitcast(E5M2), scales=dc_scales[:, cols], in_=turned[:])
+
+        for b in range(BLOCKS):
+            codes, scales = gather_and_quantise(u_tables[b], user_list, f"u{b}")
+            acc = sums.tile([P, SLOTS], F32, name="acc")
+            nc.tensor.matmul_mx(
+                out=acc[:], lhsT=codes[:].bitcast(E4M3), lhsT_scale=scales[:],
+                rhs=dc_codes[:].bitcast(E5M2), rhs_scale=dc_scales[:], start=True, stop=True,
+            )
+            result = keep.tile([P, SLOTS], F32, name=f"result{b}")
+            nc.scalar.copy(out=result[:], in_=acc[:])
+            nc.sync.dma_start(out=out[b * P : (b + 1) * P, :], in_=result[:])

@@ -15,6 +15,7 @@ P = 128
 SLOTS = 512
 TABLE = 2048
 BLOCKS = 4
+WINDOW_BYTES = 4 * TABLE
 
 FLOPS = 2 * 2 * 512 * 512 * 512
 BYTES = 4 * (2 * 512 * 2048 + 2 * 512 * 512 + 2048) + 2 * 2 * 128 * 32
@@ -24,55 +25,107 @@ def tile_attend_gbil_R_kernel(tc, G, uT, vT, su, uoffs, offs, out):
     nc = tc.nc
     with ExitStack() as ctx:
         keep = ctx.enter_context(tc.tile_pool(name="keep", bufs=1))
+        placed = ctx.enter_context(tc.tile_pool(name="placed", bufs=1))
         turn = ctx.enter_context(tc.psum_pool(name="turn", bufs=4))
-        sums = ctx.enter_context(tc.psum_pool(name="sums", bufs=4))
+        spread = ctx.enter_context(tc.psum_pool(name="spread", bufs=1))
+        sums = ctx.enter_context(tc.psum_pool(name="sums", bufs=3))
+
+        def place(at, shape, dtype, name):
+            return placed.tile(shape, dtype, name=name, offset=at, align_bytes=64)
+
+        def window_at(b):
+            return b * WINDOW_BYTES
+
+        g_rows_at = window_at(8)
+        g_k_at = window_at(9)
+        dc_k_at = g_k_at + 4096
+
+        def turned_at(b):
+            return window_at(10) + 1024 * b
+
+        def load_window(b):
+            window = place(window_at(b), [P, TABLE], F32, f"window{b}")
+            source = vT if b < BLOCKS else uT
+            rows = slice((b % BLOCKS) * P, (b % BLOCKS + 1) * P)
+            nc.sync.dma_start(out=window[:], in_=source[rows, :])
+            return window
 
         su_first = keep.tile([1, TABLE], F32, name="su_first")
         nc.sync.dma_start(out=su_first[:], in_=su[0:1, :])
-        g_rows = keep.tile([P, 4 * SLOTS], F32, name="g_rows")
+        g_rows = place(g_rows_at, [P, 4 * SLOTS], F32, "g_rows")
         nc.sync.dma_start(out=g_rows[:], in_=G.rearrange("(m j) i -> m (j i)", j=4))
         item_list = keep.tile([P, SLOTS // 16], U16, name="item_list")
         nc.sync.dma_start(item_list[:], offs)
         user_list = keep.tile([P, SLOTS // 16], U16, name="user_list")
         nc.sync.dma_start(user_list[:], uoffs)
+        windows = [load_window(b) for b in range(2 * BLOCKS)]
 
         su_table = keep.tile([P, TABLE], F32, name="su_table")
         nc.vector.memset(su_table[:], 0.0)
         nc.vector.tensor_copy(out=su_table[0:1, :], in_=su_first[:])
 
-        v_tables, u_tables = [], []
-        for b in range(BLOCKS):
-            table = keep.tile([P, TABLE], F32, name=f"v_table{b}")
-            nc.sync.dma_start(out=table[:], in_=vT[b * P : (b + 1) * P, :])
-            v_tables.append(table)
-        for b in range(BLOCKS):
-            table = keep.tile([P, TABLE], F32, name=f"u_table{b}")
-            nc.sync.dma_start(out=table[:], in_=uT[b * P : (b + 1) * P, :])
-            u_tables.append(table)
-
         ident = keep.tile([P, P], F32, name="ident")
         make_identity(nc, ident[:])
 
-        su_row = keep.tile([P, SLOTS], F32, name="su_row")
-        nc.vector.tensor_copy(su_row[:], su_table[:].indirect(user_list[:]))
-        bank = turn.tile([P, 4, P], F32, name="bank")
-        for k in range(4):
-            nc.tensor.transpose(bank[:, k, :], su_row[:, k * P : (k + 1) * P], ident[:])
-        su_cols = keep.tile([P, 4], F32, name="su_cols")
-        nc.scalar.copy(out=su_cols[:], in_=bank[:, :, 0])
-        bank = turn.tile([P, 4, P], F32, name="bank")
-        for k in range(4):
-            nc.tensor.transpose(bank[:, k, :], su_cols[:, k : k + 1].to_broadcast([P, P]), ident[:])
-        su_wide = keep.tile([P, SLOTS], F32, name="su_wide")
-        nc.scalar.copy(
-            out=su_wide[:].rearrange("p (u m e) -> p u m e", u=2, e=2),
-            in_=bank[:].rearrange("p k n -> p (k n)").rearrange("p (m u e) -> p u m e", u=2, e=2),
-        )
+        def turn_words(words0, words1, turned):
+            bank = turn.tile([P, 4, P], F32, name="bank")
+            nc.tensor.transpose(bank[:, 0, :], words0, ident[:])
+            nc.tensor.transpose(bank[:, 1, :], words1, ident[:])
+            nc.scalar.copy(
+                out=turned.bitcast(F32).rearrange("p (n u) -> p n u", u=2),
+                in_=bank[:, 0:2, :].rearrange("p u n -> p n u"),
+            )
+
+        turned, packed, accs, su_wide = {}, {}, {}, {}
+
+        def gather(b, at):
+            offsets = item_list if b < BLOCKS else user_list
+            picked = place(at, [P, SLOTS], BF16, f"picked{b}")
+            nc.vector.tensor_copy(picked[:], windows[b][:].indirect(offsets[:]))
+            words = picked[:].bitcast(F32)
+            turned[b] = place(turned_at(b), [P, 4 * P], BF16, f"turned{b}")
+            turn_words(words[:, 0:256:2], words[:, 1:256:2], turned[b][:])
+
+        def quantise(b, at):
+            codes = place(at, [P, P], U32, f"codes{b}")
+            scales = place(at + 512, [P, P], U8, f"scales{b}")
+            nc.vector.quantize_mx(out=codes[:].bitcast(E4M3), scales=scales[:], in_=turned[b][:])
+            packed[b] = (codes, scales)
+
+        def multiply(b, rhs_codes, rhs_scales):
+            codes, scales = packed[b]
+            accs[b] = sums.tile([P, SLOTS], F32, name="acc")
+            nc.tensor.matmul_mx(
+                out=accs[b][:], lhsT=codes[:].bitcast(E4M3), lhsT_scale=scales[:],
+                rhs=rhs_codes[:].bitcast(E5M2), rhs_scale=rhs_scales[:], start=True, stop=True,
+            )
+
+        def su_at(b):
+            return window_at(b + 1) + 4096 if b else window_at(0) + 4096
+
+        def spread_su(b):
+            su_wide[b] = place(su_at(b), [P, SLOTS], F32, f"su_wide{b}")
+            nc.scalar.copy(
+                out=su_wide[b][:].rearrange("p (u m e) -> p u m e", u=2, e=2),
+                in_=su_bank[:].rearrange("p k n -> p (k n)").rearrange("p (m u e) -> p u m e", u=2, e=2),
+            )
+
+        def scale_and_turn(b):
+            dc = place(window_at(b + 2) + 1024, [P, SLOTS], BF16, f"dc{b}")
+            nc.vector.tensor_tensor(dc[:], accs[b][:], su_wide[0][:], mybir.AluOpType.mult)
+            words = dc[:].bitcast(F32)
+            turn_words(words[:, 0:P], words[:, P : 2 * P], dc_k[:, b * SLOTS : (b + 1) * SLOTS])
+
+        def store(b):
+            result = keep.tile([P, SLOTS], F32, name=f"result{b}")
+            nc.scalar.copy(out=result[:], in_=accs[b][:])
+            d = b - BLOCKS
+            nc.sync.dma_start(out=out[d * P : (d + 1) * P, :], in_=result[:])
 
         g_bf = keep.tile([P, 4 * SLOTS], BF16, name="g_bf", align_bytes=64)
         nc.vector.tensor_copy(out=g_bf[:], in_=g_rows[:])
         g_words = g_bf[:].bitcast(F32)
-        g_k = keep.tile([P, 4 * SLOTS], BF16, name="g_k", align_bytes=64)
+        g_k = place(g_k_at, [P, 4 * SLOTS], BF16, "g_k")
         for h in range(2):
             bank = turn.tile([P, 4, P], F32, name="bank")
             for e in range(2):
@@ -83,54 +136,44 @@ def tile_attend_gbil_R_kernel(tc, G, uT, vT, su, uoffs, offs, out):
                 out=g_k[:].bitcast(F32)[:, 512 * h : 512 * (h + 1)].rearrange("p (m x) -> p m x", x=4),
                 in_=bank[:].rearrange("p x m -> p m x"),
             )
+        su_row = keep.tile([P, SLOTS], F32, name="su_row")
+        nc.vector.tensor_copy(su_row[:], su_table[:].indirect(user_list[:]))
+        gather(0, turned_at(8))
+        bank = turn.tile([P, 4, P], F32, name="bank")
+        for k in range(4):
+            nc.tensor.transpose(bank[:, k, :], su_row[:, k * P : (k + 1) * P], ident[:])
+        su_cols = keep.tile([P, 4], F32, name="su_cols")
+        nc.scalar.copy(out=su_cols[:], in_=bank[:, :, 0])
+        su_bank = spread.tile([P, 4, P], F32, name="su_bank")
+        for k in range(4):
+            nc.tensor.transpose(su_bank[:, k, :], su_cols[:, k : k + 1].to_broadcast([P, P]), ident[:])
+        spread_su(0)
+
         g_codes = keep.tile([P, SLOTS], U32, name="g_codes", align_bytes=64)
-        g_scales = keep.tile([P, SLOTS], U8, name="g_scales", align_bytes=64)
+        g_scales = place(window_at(0), [P, SLOTS], U8, "g_scales")
         nc.vector.quantize_mx(out=g_codes[:].bitcast(E5M2), scales=g_scales[:], in_=g_k[:])
+        gather(1, g_rows_at)
+        quantise(0, window_at(1))
+        multiply(0, g_codes, g_scales)
 
-        def turn_words(words0, words1, name):
-            bank = turn.tile([P, 4, P], F32, name="bank")
-            nc.tensor.transpose(bank[:, 0, :], words0, ident[:])
-            nc.tensor.transpose(bank[:, 1, :], words1, ident[:])
-            turned = keep.tile([P, 4 * P], BF16, name=name, align_bytes=64)
-            nc.scalar.copy(
-                out=turned[:].bitcast(F32).rearrange("p (n u) -> p n u", u=2),
-                in_=bank[:, 0:2, :].rearrange("p u n -> p n u"),
-            )
-            return turned
-
-        def gather_and_quantise(table, offsets, name):
-            picked = keep.tile([P, SLOTS], BF16, name=name + "_picked", align_bytes=64)
-            nc.vector.tensor_copy(picked[:], table[:].indirect(offsets[:]))
-            words = picked[:].bitcast(F32)
-            turned = turn_words(words[:, 0:256:2], words[:, 1:256:2], name + "_turned")
-            codes = keep.tile([P, P], U32, name=name + "_codes", align_bytes=64)
-            scales = keep.tile([P, P], U8, name=name + "_scales", align_bytes=64)
-            nc.vector.quantize_mx(out=codes[:].bitcast(E4M3), scales=scales[:], in_=turned[:])
-            return codes, scales
-
-        dc_codes = keep.tile([P, SLOTS], U32, name="dc_codes", align_bytes=64)
-        dc_scales = keep.tile([P, SLOTS], U8, name="dc_scales", align_bytes=64)
-        for b in range(BLOCKS):
-            codes, scales = gather_and_quantise(v_tables[b], item_list, f"v{b}")
-            acc = sums.tile([P, SLOTS], F32, name="acc")
-            nc.tensor.matmul_mx(
-                out=acc[:], lhsT=codes[:].bitcast(E4M3), lhsT_scale=scales[:],
-                rhs=g_codes[:].bitcast(E5M2), rhs_scale=g_scales[:], start=True, stop=True,
-            )
-            dc = keep.tile([P, SLOTS], BF16, name=f"dc{b}", align_bytes=64)
-            nc.vector.tensor_tensor(dc[:], acc[:], su_wide[:], mybir.AluOpType.mult)
-            words = dc[:].bitcast(F32)
-            turned = turn_words(words[:, 0:P], words[:, P : 2 * P], f"dc{b}_turned")
-            cols = slice(b * P, (b + 1) * P)
-            nc.vector.quantize_mx(out=dc_codes[:, cols].bitcast(E5M2), scales=dc_scales[:, cols], in_=turned[:])
-
-        for b in range(BLOCKS):
-            codes, scales = gather_and_quantise(u_tables[b], user_list, f"u{b}")
-            acc = sums.tile([P, SLOTS], F32, name="acc")
-            nc.tensor.matmul_mx(
-                out=acc[:], lhsT=codes[:].bitcast(E4M3), lhsT_scale=scales[:],
-                rhs=dc_codes[:].bitcast(E5M2), rhs_scale=dc_scales[:], start=True, stop=True,
-            )
-            result = keep.tile([P, SLOTS], F32, name=f"result{b}")
-            nc.scalar.copy(out=result[:], in_=acc[:])
-            nc.sync.dma_start(out=out[b * P : (b + 1) * P, :], in_=result[:])
+        dc_k = place(dc_k_at, [P, 4 * SLOTS], BF16, "dc_k")
+        for b in range(2, 6):
+            gather(b, window_at(12) + 1024 * b)
+            scale_and_turn(b - 2)
+            quantise(b - 1, window_at(b))
+            if b <= BLOCKS:
+                multiply(b - 1, g_codes, g_scales)
+        gather(6, window_at(12) + 1024 * 6)
+        dc_codes = place(window_at(6), [P, SLOTS], U32, "dc_codes")
+        dc_scales = place(window_at(6) + 2048, [P, SLOTS], U8, "dc_scales")
+        nc.vector.quantize_mx(out=dc_codes[:].bitcast(E5M2), scales=dc_scales[:], in_=dc_k[:])
+        multiply(4, dc_codes, dc_scales)
+        store(4)
+        quantise(5, window_at(6) + 4096)
+        multiply(5, dc_codes, dc_scales)
+        store(5)
+        gather(7, window_at(12) + 1024 * 7)
+        for b in (6, 7):
+            quantise(b, window_at(7) + 1024 * (b - 6))
+            multiply(b, dc_codes, dc_scales)
+            store(b)

@@ -10,12 +10,15 @@ U16 = mybir.dt.uint16
 U8 = mybir.dt.uint8
 E4M3 = mybir.dt.float8_e4m3fn_x4
 E5M2 = mybir.dt.float8_e5m2_x4
+COPY = mybir.ActivationFunctionType.Copy
 
 P = 128
 SLOTS = 512
 TABLE = 2048
 BLOCKS = 4
 WINDOW_BYTES = 4 * TABLE
+VECTOR_SLOTS = 288
+SU_VECTOR_SLOTS = 256
 
 FLOPS = 2 * 2 * 512 * 512 * 512
 BYTES = 4 * (2 * 512 * 2048 + 2 * 512 * 512 + 2048) + 2 * 2 * 128 * 32
@@ -26,154 +29,147 @@ def tile_attend_gbil_R_kernel(tc, G, uT, vT, su, uoffs, offs, out):
     with ExitStack() as ctx:
         keep = ctx.enter_context(tc.tile_pool(name="keep", bufs=1))
         placed = ctx.enter_context(tc.tile_pool(name="placed", bufs=1))
-        turn = ctx.enter_context(tc.psum_pool(name="turn", bufs=4))
-        spread = ctx.enter_context(tc.psum_pool(name="spread", bufs=1))
+        head = ctx.enter_context(tc.psum_pool(name="head", bufs=1))
+        turn = ctx.enter_context(tc.psum_pool(name="turn", bufs=3))
         sums = ctx.enter_context(tc.psum_pool(name="sums", bufs=3))
 
-        def place(at, shape, dtype, name):
-            return placed.tile(shape, dtype, name=name, offset=at, align_bytes=64)
-
-        def window_at(b):
-            return b * WINDOW_BYTES
-
-        g_rows_at = window_at(8)
-        g_k_at = window_at(9)
-        dc_k_at = g_k_at + 4096
-
-        def turned_at(b):
-            return window_at(10) + 1024 * b
-
-        def load_window(b):
-            window = place(window_at(b), [P, TABLE], F32, f"window{b}")
-            source = vT if b < BLOCKS else uT
-            rows = slice((b % BLOCKS) * P, (b % BLOCKS + 1) * P)
-            nc.sync.dma_start(out=window[:], in_=source[rows, :])
-            return window
-
-        su_first = keep.tile([1, TABLE], F32, name="su_first")
-        nc.sync.dma_start(out=su_first[:], in_=su[0:1, :])
-        g_rows = place(g_rows_at, [P, 4 * SLOTS], F32, "g_rows")
-        nc.sync.dma_start(out=g_rows[:], in_=G.rearrange("(m j) i -> m (j i)", j=4))
-        item_list = keep.tile([P, SLOTS // 16], U16, name="item_list")
-        nc.sync.dma_start(item_list[:], offs)
-        user_list = keep.tile([P, SLOTS // 16], U16, name="user_list")
-        nc.sync.dma_start(user_list[:], uoffs)
-        windows = [load_window(b) for b in range(2 * BLOCKS)]
+        def on_window(b, shape, dtype, name, at=0):
+            if b >= 2 * BLOCKS:
+                return keep.tile(shape, dtype, name=name, align_bytes=64)
+            return placed.tile(shape, dtype, name=name, offset=b * WINDOW_BYTES + at, align_bytes=64)
 
         su_table = keep.tile([P, TABLE], F32, name="su_table")
-        nc.vector.memset(su_table[:], 0.0)
-        nc.vector.tensor_copy(out=su_table[0:1, :], in_=su_first[:])
+        nc.vector.memset(su_table[:].bitcast(U32), 0)
+        g_rows = keep.tile([P, 4 * SLOTS], F32, name="g_rows")
+        nc.sync.dma_start(out=g_rows[:], in_=G.rearrange("(m j) i -> m (j i)", j=4))
+        user_list = keep.tile([P, SLOTS // 16], U16, name="user_list")
+        item_list = keep.tile([P, SLOTS // 16], U16, name="item_list")
+        nc.sync.dma_start(item_list[:], offs)
+        windows = []
+        for b in range(2 * BLOCKS):
+            window = on_window(b, [P, TABLE], F32, f"window{b}")
+            source = vT if b < BLOCKS else uT
+            nc.sync.dma_start(out=window[:], in_=source[(b % BLOCKS) * P : (b % BLOCKS + 1) * P, :])
+            windows.append(window)
+            if b == 0:
+                nc.sync.dma_start(out=su_table[0:1, :], in_=su[0:1, :])
+                nc.sync.dma_start(user_list[:], uoffs)
 
         ident = keep.tile([P, P], F32, name="ident")
         make_identity(nc, ident[:])
 
-        def turn_words(words0, words1, turned):
-            bank = turn.tile([P, 4, P], F32, name="bank")
-            nc.tensor.transpose(bank[:, 0, :], words0, ident[:])
-            nc.tensor.transpose(bank[:, 1, :], words1, ident[:])
+
+        g_bf = keep.tile([P, 4 * SLOTS], BF16, name="g_bf", align_bytes=64)
+        g_k = keep.tile([P, 4 * SLOTS], BF16, name="g_k", align_bytes=64)
+        for h in range(2):
+            half = slice(2 * SLOTS * h, 2 * SLOTS * (h + 1))
+            if h == 0:
+                nc.vector.tensor_copy(out=g_bf[:, half], in_=g_rows[:, half])
+            else:
+                nc.scalar.activation(g_bf[:, half], g_rows[:, half], COPY)
+            words = g_bf[:, half].bitcast(F32)
+            bank = head.tile([P, 4, P], F32, name=f"g_bank{h}")
+            for e in range(2):
+                for u in range(2):
+                    nc.tensor.transpose(bank[:, 2 * e + u, :], words[:, 256 * e + u : 256 * (e + 1) : 2], ident[:])
             nc.scalar.copy(
-                out=turned.bitcast(F32).rearrange("p (n u) -> p n u", u=2),
+                out=g_k[:, half].bitcast(F32).rearrange("p (e m u) -> p e m u", e=2, u=2),
+                in_=bank[:].rearrange("p (e u) m -> p e m u", u=2),
+            )
+        g_codes = keep.tile([P, SLOTS], U32, name="g_codes", align_bytes=64)
+        g_scales = keep.tile([P, SLOTS], U8, name="g_scales", align_bytes=64)
+        nc.vector.quantize_mx(out=g_codes[:].bitcast(E5M2), scales=g_scales[:], in_=g_k[:])
+
+        su_cols = on_window(1, [P, 1, 4], F32, "su_cols", 4096)
+
+        def gather_su():
+            su_row = on_window(0, [P, SLOTS], F32, "su_row")
+            cut = SU_VECTOR_SLOTS // 16
+            nc.vector.tensor_copy(su_row[:, :SU_VECTOR_SLOTS], su_table[:].indirect(user_list[:, :cut]))
+            nc.scalar.activation(su_row[:, SU_VECTOR_SLOTS:], su_table[:].indirect(user_list[:, cut:]), COPY)
+            bank = head.tile([P, 4, P], F32, name="g_bank0")
+            for j in range(4):
+                nc.tensor.transpose(bank[:, j, :], su_row[:, j:SLOTS:4], ident[:])
+            nc.scalar.copy(out=su_cols[:, 0, :], in_=bank[:, :, 0])
+
+        dc_codes = keep.tile([P, SLOTS], U32, name="dc_codes", align_bytes=64)
+        dc_scales = keep.tile([P, SLOTS], U8, name="dc_scales", align_bytes=64)
+        turned, accs = {}, {}
+
+        def gather(b):
+            offsets = item_list if b < BLOCKS else user_list
+            picked = keep.tile([P, SLOTS], BF16, name=f"picked{b}")
+            cut = VECTOR_SLOTS // 16
+            nc.vector.tensor_copy(picked[:, :VECTOR_SLOTS], windows[b][:].indirect(offsets[:, :cut]))
+            nc.scalar.activation(picked[:, VECTOR_SLOTS:], windows[b][:].indirect(offsets[:, cut:]), COPY)
+            words = picked[:].bitcast(F32)
+            bank = turn.tile([P, 4, P], F32, name="bank")
+            for u in range(2):
+                nc.tensor.transpose(bank[:, u, :], words[:, u:256:2], ident[:])
+            turned[b] = keep.tile([P, 4 * P], BF16, name=f"turned{b}", align_bytes=64)
+            nc.scalar.copy(
+                out=turned[b][:].bitcast(F32).rearrange("p (n u) -> p n u", u=2),
                 in_=bank[:, 0:2, :].rearrange("p u n -> p n u"),
             )
 
-        turned, packed, accs, su_wide = {}, {}, {}, {}
-
-        def gather(b, at):
-            offsets = item_list if b < BLOCKS else user_list
-            picked = place(at, [P, SLOTS], BF16, f"picked{b}")
-            nc.vector.tensor_copy(picked[:], windows[b][:].indirect(offsets[:]))
-            words = picked[:].bitcast(F32)
-            turned[b] = place(turned_at(b), [P, 4 * P], BF16, f"turned{b}")
-            turn_words(words[:, 0:256:2], words[:, 1:256:2], turned[b][:])
-
-        def quantise(b, at):
-            codes = place(at, [P, P], U32, f"codes{b}")
-            scales = place(at + 512, [P, P], U8, f"scales{b}")
+        def multiply(b):
+            codes = on_window(b + 1, [P, P], U32, f"codes{b}")
+            scales = on_window(b + 1, [P, P], U8, f"scales{b}", 512)
             nc.vector.quantize_mx(out=codes[:].bitcast(E4M3), scales=scales[:], in_=turned[b][:])
-            packed[b] = (codes, scales)
-
-        def multiply(b, rhs_codes, rhs_scales):
-            codes, scales = packed[b]
             accs[b] = sums.tile([P, SLOTS], F32, name="acc")
-            nc.tensor.matmul_mx(
-                out=accs[b][:], lhsT=codes[:].bitcast(E4M3), lhsT_scale=scales[:],
-                rhs=rhs_codes[:].bitcast(E5M2), rhs_scale=rhs_scales[:], start=True, stop=True,
-            )
+            if b < BLOCKS:
+                for j in range(4):
+                    cols = slice(j * P, (j + 1) * P)
+                    nc.tensor.matmul_mx(
+                        out=accs[b][:, cols], lhsT=g_codes[:, cols].bitcast(E5M2), lhsT_scale=g_scales[:, cols],
+                        rhs=codes[:].bitcast(E4M3), rhs_scale=scales[:], start=True, stop=True,
+                    )
+            elif b == 2 * BLOCKS - 1:
+                accs[b + 1] = sums.tile([P, SLOTS], F32, name="acc")
+                for h in range(2):
+                    cols = slice(h * 2 * P, (h + 1) * 2 * P)
+                    nc.tensor.matmul_mx(
+                        out=accs[b + h][:, : 2 * P], lhsT=codes[:].bitcast(E4M3), lhsT_scale=scales[:],
+                        rhs=dc_codes[:, cols].bitcast(E5M2), rhs_scale=dc_scales[:, cols], start=True, stop=True,
+                    )
+            else:
+                nc.tensor.matmul_mx(
+                    out=accs[b][:], lhsT=codes[:].bitcast(E4M3), lhsT_scale=scales[:],
+                    rhs=dc_codes[:].bitcast(E5M2), rhs_scale=dc_scales[:], start=True, stop=True,
+                )
 
-        def su_at(b):
-            return window_at(b + 1) + 4096 if b else window_at(0) + 4096
+        def finish(b):
+            if b < BLOCKS:
+                dc = on_window(b + 2, [P, P, 4], BF16, f"dc{b}", 1024)
+                nc.vector.tensor_tensor(
+                    dc[:], accs[b][:].rearrange("p (j f) -> p f j", j=4), su_cols[:].to_broadcast([P, P, 4]),
+                    mybir.AluOpType.mult,
+                )
+                cols = slice(b * P, (b + 1) * P)
+                nc.vector.quantize_mx(
+                    out=dc_codes[:, cols].bitcast(E5M2), scales=dc_scales[:, cols],
+                    in_=dc[:].rearrange("p f j -> p (f j)"),
+                )
+            else:
+                result = on_window(b + 2, [P, SLOTS], F32, f"result{b}", 1024)
+                if b == 2 * BLOCKS - 1:
+                    nc.vector.tensor_copy(out=result[:, : 2 * P], in_=accs[b][:, : 2 * P])
+                    nc.scalar.copy(out=result[:, 2 * P :], in_=accs[b + 1][:, : 2 * P])
+                elif b == 2 * BLOCKS - 2:
+                    nc.scalar.copy(out=result[:], in_=accs[b][:])
+                else:
+                    nc.vector.tensor_copy(out=result[:], in_=accs[b][:])
+                d = b - BLOCKS
+                nc.sync.dma_start(out=out[d * P : (d + 1) * P, :], in_=result[:])
 
-        def spread_su(b):
-            su_wide[b] = place(su_at(b), [P, SLOTS], F32, f"su_wide{b}")
-            nc.scalar.copy(
-                out=su_wide[b][:].rearrange("p (u m e) -> p u m e", u=2, e=2),
-                in_=su_bank[:].rearrange("p k n -> p (k n)").rearrange("p (m u e) -> p u m e", u=2, e=2),
-            )
-
-        def scale_and_turn(b):
-            dc = place(window_at(b + 2) + 1024, [P, SLOTS], BF16, f"dc{b}")
-            nc.vector.tensor_tensor(dc[:], accs[b][:], su_wide[0][:], mybir.AluOpType.mult)
-            words = dc[:].bitcast(F32)
-            turn_words(words[:, 0:P], words[:, P : 2 * P], dc_k[:, b * SLOTS : (b + 1) * SLOTS])
-
-        def store(b):
-            result = keep.tile([P, SLOTS], F32, name=f"result{b}")
-            nc.scalar.copy(out=result[:], in_=accs[b][:])
-            d = b - BLOCKS
-            nc.sync.dma_start(out=out[d * P : (d + 1) * P, :], in_=result[:])
-
-        g_bf = keep.tile([P, 4 * SLOTS], BF16, name="g_bf", align_bytes=64)
-        nc.vector.tensor_copy(out=g_bf[:], in_=g_rows[:])
-        g_words = g_bf[:].bitcast(F32)
-        g_k = place(g_k_at, [P, 4 * SLOTS], BF16, "g_k")
-        for h in range(2):
-            bank = turn.tile([P, 4, P], F32, name="bank")
-            for e in range(2):
-                j = 2 * h + e
-                for u in range(2):
-                    nc.tensor.transpose(bank[:, 2 * e + u, :], g_words[:, 256 * j + u : 256 * (j + 1) : 2], ident[:])
-            nc.scalar.copy(
-                out=g_k[:].bitcast(F32)[:, 512 * h : 512 * (h + 1)].rearrange("p (m x) -> p m x", x=4),
-                in_=bank[:].rearrange("p x m -> p m x"),
-            )
-        su_row = keep.tile([P, SLOTS], F32, name="su_row")
-        nc.vector.tensor_copy(su_row[:], su_table[:].indirect(user_list[:]))
-        gather(0, turned_at(8))
-        bank = turn.tile([P, 4, P], F32, name="bank")
-        for k in range(4):
-            nc.tensor.transpose(bank[:, k, :], su_row[:, k * P : (k + 1) * P], ident[:])
-        su_cols = keep.tile([P, 4], F32, name="su_cols")
-        nc.scalar.copy(out=su_cols[:], in_=bank[:, :, 0])
-        su_bank = spread.tile([P, 4, P], F32, name="su_bank")
-        for k in range(4):
-            nc.tensor.transpose(su_bank[:, k, :], su_cols[:, k : k + 1].to_broadcast([P, P]), ident[:])
-        spread_su(0)
-
-        g_codes = keep.tile([P, SLOTS], U32, name="g_codes", align_bytes=64)
-        g_scales = place(window_at(0), [P, SLOTS], U8, "g_scales")
-        nc.vector.quantize_mx(out=g_codes[:].bitcast(E5M2), scales=g_scales[:], in_=g_k[:])
-        gather(1, g_rows_at)
-        quantise(0, window_at(1))
-        multiply(0, g_codes, g_scales)
-
-        dc_k = place(dc_k_at, [P, 4 * SLOTS], BF16, "dc_k")
-        for b in range(2, 6):
-            gather(b, window_at(12) + 1024 * b)
-            scale_and_turn(b - 2)
-            quantise(b - 1, window_at(b))
-            if b <= BLOCKS:
-                multiply(b - 1, g_codes, g_scales)
-        gather(6, window_at(12) + 1024 * 6)
-        dc_codes = place(window_at(6), [P, SLOTS], U32, "dc_codes")
-        dc_scales = place(window_at(6) + 2048, [P, SLOTS], U8, "dc_scales")
-        nc.vector.quantize_mx(out=dc_codes[:].bitcast(E5M2), scales=dc_scales[:], in_=dc_k[:])
-        multiply(4, dc_codes, dc_scales)
-        store(4)
-        quantise(5, window_at(6) + 4096)
-        multiply(5, dc_codes, dc_scales)
-        store(5)
-        gather(7, window_at(12) + 1024 * 7)
-        for b in (6, 7):
-            quantise(b, window_at(7) + 1024 * (b - 6))
-            multiply(b, dc_codes, dc_scales)
-            store(b)
+        for b in range(2 * BLOCKS + 2):
+            if b < 2 * BLOCKS:
+                gather(b)
+            if b == 1:
+                gather_su()
+            if b == BLOCKS + 1:
+                finish(b - 2)
+            if 1 <= b <= 2 * BLOCKS:
+                multiply(b - 1)
+            if b >= 2 and b != BLOCKS + 1:
+                finish(b - 2)

@@ -137,6 +137,13 @@ def tile_attend_gbil_R_kernel(tc, G, uT, vT, su, uoffs, offs, out):
                     out=accs[b][:], lhsT=codes[:].bitcast(E4M3), lhsT_scale=scales[:],
                     rhs=dc_codes[:].bitcast(E5M2), rhs_scale=dc_scales[:], start=True, stop=True,
                 )
+                if b == 2 * BLOCKS - 3:
+                    for h in range(2):
+                        spare = head.tile([P, SLOTS], F32, name=f"g_bank{h}")
+                        nc.tensor.matmul_mx(
+                            out=spare[:], lhsT=codes[:].bitcast(E4M3), lhsT_scale=scales[:],
+                            rhs=dc_codes[:].bitcast(E5M2), rhs_scale=dc_scales[:], start=True, stop=True,
+                        )
 
         def finish(b):
             if b < BLOCKS:

@@ -77,8 +77,7 @@ def tile_attend_gbil_R_kernel(tc, G, uT, vT, su, uoffs, offs, out):
                 in_=bank[:].rearrange("p (e u) m -> p e m u", u=2),
             )
         g_codes = keep.tile([P, SLOTS], U32, name="g_codes", align_bytes=64)
-        g_scales = keep.tile([P, SLOTS], U8, name="g_scales", align_bytes=64)
-        nc.vector.quantize_mx(out=g_codes[:].bitcast(E5M2), scales=g_scales[:], in_=g_k[:])
+        g_scales = on_window(0, [P, SLOTS], U8, "g_scales", 4096)
 
         su_cols = on_window(1, [P, 1, 4], F32, "su_cols", 4096)
 
@@ -94,7 +93,7 @@ def tile_attend_gbil_R_kernel(tc, G, uT, vT, su, uoffs, offs, out):
 
         dc_codes = keep.tile([P, SLOTS], U32, name="dc_codes", align_bytes=64)
         dc_scales = keep.tile([P, SLOTS], U8, name="dc_scales", align_bytes=64)
-        turned, accs = {}, {}
+        turned, packed, accs, scaled = {}, {}, {}, {}
 
         def gather(b):
             offsets = item_list if b < BLOCKS else user_list
@@ -112,10 +111,14 @@ def tile_attend_gbil_R_kernel(tc, G, uT, vT, su, uoffs, offs, out):
                 in_=bank[:, 0:2, :].rearrange("p u n -> p n u"),
             )
 
-        def multiply(b):
+        def quantise(b):
             codes = on_window(b + 1, [P, P], U32, f"codes{b}")
             scales = on_window(b + 1, [P, P], U8, f"scales{b}", 512)
             nc.vector.quantize_mx(out=codes[:].bitcast(E4M3), scales=scales[:], in_=turned[b][:])
+            packed[b] = codes, scales
+
+        def multiply(b):
+            codes, scales = packed[b]
             accs[b] = sums.tile([P, SLOTS], F32, name="acc")
             if b < BLOCKS:
                 for j in range(4):
@@ -145,6 +148,13 @@ def tile_attend_gbil_R_kernel(tc, G, uT, vT, su, uoffs, offs, out):
                             rhs=dc_codes[:].bitcast(E5M2), rhs_scale=dc_scales[:], start=True, stop=True,
                         )
 
+        def quantise_dc(b):
+            cols = slice(b * P, (b + 1) * P)
+            nc.vector.quantize_mx(
+                out=dc_codes[:, cols].bitcast(E5M2), scales=dc_scales[:, cols],
+                in_=scaled[b][:].rearrange("p f j -> p (f j)"),
+            )
+
         def finish(b):
             if b < BLOCKS:
                 dc = on_window(b + 2, [P, P, 4], BF16, f"dc{b}", 1024)
@@ -152,17 +162,13 @@ def tile_attend_gbil_R_kernel(tc, G, uT, vT, su, uoffs, offs, out):
                     dc[:], accs[b][:].rearrange("p (j f) -> p f j", j=4), su_cols[:].to_broadcast([P, P, 4]),
                     mybir.AluOpType.mult,
                 )
-                cols = slice(b * P, (b + 1) * P)
-                nc.vector.quantize_mx(
-                    out=dc_codes[:, cols].bitcast(E5M2), scales=dc_scales[:, cols],
-                    in_=dc[:].rearrange("p f j -> p (f j)"),
-                )
+                scaled[b] = dc
             else:
                 result = on_window(b + 2, [P, SLOTS], F32, f"result{b}", 1024)
                 if b == 2 * BLOCKS - 1:
                     nc.vector.tensor_copy(out=result[:, : 2 * P], in_=accs[b][:, : 2 * P])
                     nc.scalar.copy(out=result[:, 2 * P :], in_=accs[b + 1][:, : 2 * P])
-                elif b == 2 * BLOCKS - 2:
+                elif b % 2 == 0:
                     nc.scalar.copy(out=result[:], in_=accs[b][:])
                 else:
                     nc.vector.tensor_copy(out=result[:], in_=accs[b][:])
@@ -172,11 +178,17 @@ def tile_attend_gbil_R_kernel(tc, G, uT, vT, su, uoffs, offs, out):
         for b in range(2 * BLOCKS + 2):
             if b < 2 * BLOCKS:
                 gather(b)
+            if b == 0:
+                nc.vector.quantize_mx(out=g_codes[:].bitcast(E5M2), scales=g_scales[:], in_=g_k[:])
             if b == 1:
                 gather_su()
-            if b == BLOCKS + 1:
+            if 2 <= b <= BLOCKS + 1:
                 finish(b - 2)
             if 1 <= b <= 2 * BLOCKS:
+                quantise(b - 1)
+            if 2 <= b <= BLOCKS + 1:
+                quantise_dc(b - 2)
+            if 1 <= b <= 2 * BLOCKS:
                 multiply(b - 1)
-            if b >= 2 and b != BLOCKS + 1:
+            if b > BLOCKS + 1:
                 finish(b - 2)

@@ -31,7 +31,10 @@ def tile_attend_gbil_R_kernel(tc, G, uT, vT, su, uoffs, offs, out):
         placed = ctx.enter_context(tc.tile_pool(name="placed", bufs=1))
         head = ctx.enter_context(tc.psum_pool(name="head", bufs=1))
         turn = ctx.enter_context(tc.psum_pool(name="turn", bufs=3))
-        sums = ctx.enter_context(tc.psum_pool(name="sums", bufs=3))
+        sums = ctx.enter_context(tc.psum_pool(name="sums", bufs=1))
+
+        def sum_bank(b, name):
+            return sums.tile([P, SLOTS], F32, name=name, offset=2048 * (b % 3))
 
         def on_window(b, shape, dtype, name, at=0):
             if b >= 2 * BLOCKS:
@@ -98,28 +101,31 @@ def tile_attend_gbil_R_kernel(tc, G, uT, vT, su, uoffs, offs, out):
         def gather(b):
             offsets = item_list if b < BLOCKS else user_list
             picked = keep.tile([P, SLOTS], BF16, name=f"picked{b}")
-            cut = VECTOR_SLOTS // 16
-            nc.vector.tensor_copy(picked[:, :VECTOR_SLOTS], windows[b][:].indirect(offsets[:, :cut]))
-            nc.scalar.activation(picked[:, VECTOR_SLOTS:], windows[b][:].indirect(offsets[:, cut:]), COPY)
+            share = VECTOR_SLOTS if b < 2 * BLOCKS - 1 else SLOTS // 2
+            cut = share // 16
+            nc.vector.tensor_copy(picked[:, :share], windows[b][:].indirect(offsets[:, :cut]))
+            nc.scalar.activation(picked[:, share:], windows[b][:].indirect(offsets[:, cut:]), COPY)
             words = picked[:].bitcast(F32)
             bank = turn.tile([P, 4, P], F32, name="bank")
             for u in range(2):
                 nc.tensor.transpose(bank[:, u, :], words[:, u:256:2], ident[:])
             turned[b] = keep.tile([P, 4 * P], BF16, name=f"turned{b}", align_bytes=64)
-            nc.scalar.copy(
+            copy = nc.vector.tensor_copy if b == 6 else nc.scalar.copy
+            copy(
                 out=turned[b][:].bitcast(F32).rearrange("p (n u) -> p n u", u=2),
                 in_=bank[:, 0:2, :].rearrange("p u n -> p n u"),
             )
 
         def quantise(b):
-            codes = on_window(b + 1, [P, P], U32, f"codes{b}")
-            scales = on_window(b + 1, [P, P], U8, f"scales{b}", 512)
+            held = 8 if b == 5 else b + 1
+            codes = on_window(held, [P, P], U32, f"codes{b}")
+            scales = on_window(held, [P, P], U8, f"scales{b}", 512)
             nc.vector.quantize_mx(out=codes[:].bitcast(E4M3), scales=scales[:], in_=turned[b][:])
             packed[b] = codes, scales
 
         def multiply(b):
             codes, scales = packed[b]
-            accs[b] = sums.tile([P, SLOTS], F32, name="acc")
+            accs[b] = sum_bank(b, f"acc{b}")
             if b < BLOCKS:
                 for j in range(4):
                     cols = slice(j * P, (j + 1) * P)
@@ -128,7 +134,7 @@ def tile_attend_gbil_R_kernel(tc, G, uT, vT, su, uoffs, offs, out):
                         rhs=codes[:].bitcast(E4M3), rhs_scale=scales[:], start=True, stop=True,
                     )
             elif b == 2 * BLOCKS - 1:
-                accs[b + 1] = sums.tile([P, SLOTS], F32, name="acc")
+                accs[b + 1] = sum_bank(b + 1, f"acc{b + 1}")
                 for h in range(2):
                     cols = slice(h * 2 * P, (h + 1) * 2 * P)
                     nc.tensor.matmul_mx(
@@ -140,13 +146,14 @@ def tile_attend_gbil_R_kernel(tc, G, uT, vT, su, uoffs, offs, out):
                     out=accs[b][:], lhsT=codes[:].bitcast(E4M3), lhsT_scale=scales[:],
                     rhs=dc_codes[:].bitcast(E5M2), rhs_scale=dc_scales[:], start=True, stop=True,
                 )
-                if b == 2 * BLOCKS - 3:
-                    for h in range(2):
-                        spare = head.tile([P, SLOTS], F32, name=f"g_bank{h}")
-                        nc.tensor.matmul_mx(
-                            out=spare[:], lhsT=codes[:].bitcast(E4M3), lhsT_scale=scales[:],
-                            rhs=dc_codes[:].bitcast(E5M2), rhs_scale=dc_scales[:], start=True, stop=True,
-                        )
+
+        def warm_up(b):
+            codes, scales = packed[b]
+            spare = sum_bank(b, f"spare{b}")
+            nc.tensor.matmul_mx(
+                out=spare[:], lhsT=codes[:].bitcast(E4M3), lhsT_scale=scales[:],
+                rhs=dc_codes[:].bitcast(E5M2), rhs_scale=dc_scales[:], start=True, stop=True,
+            )
 
         def quantise_dc(b):
             cols = slice(b * P, (b + 1) * P)
@@ -164,18 +171,18 @@ def tile_attend_gbil_R_kernel(tc, G, uT, vT, su, uoffs, offs, out):
                 )
                 scaled[b] = dc
             else:
-                result = on_window(b + 2, [P, SLOTS], F32, f"result{b}", 1024)
+                result = on_window(6 if b < 6 else 8, [P, SLOTS], F32, f"result{b}", 2048 * (b - 3))
                 if b == 2 * BLOCKS - 1:
                     nc.vector.tensor_copy(out=result[:, : 2 * P], in_=accs[b][:, : 2 * P])
                     nc.scalar.copy(out=result[:, 2 * P :], in_=accs[b + 1][:, : 2 * P])
-                elif b % 2 == 0:
+                elif b > BLOCKS:
                     nc.scalar.copy(out=result[:], in_=accs[b][:])
                 else:
                     nc.vector.tensor_copy(out=result[:], in_=accs[b][:])
                 d = b - BLOCKS
                 nc.sync.dma_start(out=out[d * P : (d + 1) * P, :], in_=result[:])
 
-        for b in range(2 * BLOCKS + 2):
+        for b in range(6):
             if b < 2 * BLOCKS:
                 gather(b)
             if b == 0:
@@ -190,5 +197,17 @@ def tile_attend_gbil_R_kernel(tc, G, uT, vT, su, uoffs, offs, out):
                 quantise_dc(b - 2)
             if 1 <= b <= 2 * BLOCKS:
                 multiply(b - 1)
-            if b > BLOCKS + 1:
-                finish(b - 2)
+        quantise(5)
+        multiply(5)
+        gather(6)
+        finish(4)
+        finish(5)
+        warm_up(4)
+        warm_up(5)
+        gather(7)
+        quantise(6)
+        multiply(6)
+        quantise(7)
+        multiply(7)
+        finish(6)
+        finish(7)

@@ -29,15 +29,16 @@ def tile_attend_gbil_R_kernel(tc, G, uT, vT, su, uoffs, offs, out):
     with ExitStack() as ctx:
         keep = ctx.enter_context(tc.tile_pool(name="keep", bufs=1))
         placed = ctx.enter_context(tc.tile_pool(name="placed", bufs=1))
-        head = ctx.enter_context(tc.psum_pool(name="head", bufs=1))
-        turn = ctx.enter_context(tc.psum_pool(name="turn", bufs=3))
-        sums = ctx.enter_context(tc.psum_pool(name="sums", bufs=1))
+        psum = ctx.enter_context(tc.psum_pool(name="psum", bufs=1))
+
+        def in_bank(index, shape, name):
+            return psum.tile(shape, F32, name=name, offset=2048 * index)
 
         def sum_bank(b, name):
-            return sums.tile([P, SLOTS], F32, name=name, offset=2048 * (b % 3))
+            return in_bank(5 + b % 3, [P, SLOTS], name)
 
         def on_window(b, shape, dtype, name, at=0):
-            if b >= 2 * BLOCKS:
+            if b > 2 * BLOCKS:
                 return keep.tile(shape, dtype, name=name, align_bytes=64)
             return placed.tile(shape, dtype, name=name, offset=b * WINDOW_BYTES + at, align_bytes=64)
 
@@ -71,7 +72,7 @@ def tile_attend_gbil_R_kernel(tc, G, uT, vT, su, uoffs, offs, out):
             else:
                 nc.scalar.activation(g_bf[:, half], g_rows[:, half], COPY)
             words = g_bf[:, half].bitcast(F32)
-            bank = head.tile([P, 4, P], F32, name=f"g_bank{h}")
+            bank = in_bank(h, [P, 4, P], f"g_bank{h}")
             for e in range(2):
                 for u in range(2):
                     nc.tensor.transpose(bank[:, 2 * e + u, :], words[:, 256 * e + u : 256 * (e + 1) : 2], ident[:])
@@ -89,7 +90,7 @@ def tile_attend_gbil_R_kernel(tc, G, uT, vT, su, uoffs, offs, out):
             cut = SU_VECTOR_SLOTS // 16
             nc.vector.tensor_copy(su_row[:, :SU_VECTOR_SLOTS], su_table[:].indirect(user_list[:, :cut]))
             nc.scalar.activation(su_row[:, SU_VECTOR_SLOTS:], su_table[:].indirect(user_list[:, cut:]), COPY)
-            bank = head.tile([P, 4, P], F32, name="g_bank0")
+            bank = in_bank(0, [P, 4, P], "su_bank")
             for j in range(4):
                 nc.tensor.transpose(bank[:, j, :], su_row[:, j:SLOTS:4], ident[:])
             nc.scalar.copy(out=su_cols[:, 0, :], in_=bank[:, :, 0])
@@ -106,26 +107,26 @@ def tile_attend_gbil_R_kernel(tc, G, uT, vT, su, uoffs, offs, out):
             nc.vector.tensor_copy(picked[:, :share], windows[b][:].indirect(offsets[:, :cut]))
             nc.scalar.activation(picked[:, share:], windows[b][:].indirect(offsets[:, cut:]), COPY)
             words = picked[:].bitcast(F32)
-            bank = turn.tile([P, 4, P], F32, name="bank")
+            bank = in_bank(2 + b % 3, [P, 4, P], f"bank{b}")
             for u in range(2):
                 nc.tensor.transpose(bank[:, u, :], words[:, u:256:2], ident[:])
             turned[b] = keep.tile([P, 4 * P], BF16, name=f"turned{b}", align_bytes=64)
-            copy = nc.vector.tensor_copy if b == 6 else nc.scalar.copy
-            copy(
+            nc.scalar.copy(
                 out=turned[b][:].bitcast(F32).rearrange("p (n u) -> p n u", u=2),
                 in_=bank[:, 0:2, :].rearrange("p u n -> p n u"),
             )
 
         def quantise(b):
-            held = 8 if b == 5 else b + 1
-            codes = on_window(held, [P, P], U32, f"codes{b}")
-            scales = on_window(held, [P, P], U8, f"scales{b}", 512)
+            held, at = {4: (6, 0), 5: (6, 1024), 6: (7, 4096), 7: (9, 0)}.get(b, (b + 1, 0))
+            codes = on_window(held, [P, P], U32, f"codes{b}", at)
+            scales = on_window(held, [P, P], U8, f"scales{b}", at + 512)
             nc.vector.quantize_mx(out=codes[:].bitcast(E4M3), scales=scales[:], in_=turned[b][:])
             packed[b] = codes, scales
 
         def multiply(b):
             codes, scales = packed[b]
-            accs[b] = sum_bank(b, f"acc{b}")
+            if b < 2 * BLOCKS - 1:
+                accs[b] = sum_bank(b, f"acc{b}")
             if b < BLOCKS:
                 for j in range(4):
                     cols = slice(j * P, (j + 1) * P)
@@ -134,11 +135,11 @@ def tile_attend_gbil_R_kernel(tc, G, uT, vT, su, uoffs, offs, out):
                         rhs=codes[:].bitcast(E4M3), rhs_scale=scales[:], start=True, stop=True,
                     )
             elif b == 2 * BLOCKS - 1:
-                accs[b + 1] = sum_bank(b + 1, f"acc{b + 1}")
+                accs[b] = [in_bank(index, [P, 2 * P], f"half{index}") for index in (0, 1)]
                 for h in range(2):
                     cols = slice(h * 2 * P, (h + 1) * 2 * P)
                     nc.tensor.matmul_mx(
-                        out=accs[b + h][:, : 2 * P], lhsT=codes[:].bitcast(E4M3), lhsT_scale=scales[:],
+                        out=accs[b][h][:], lhsT=codes[:].bitcast(E4M3), lhsT_scale=scales[:],
                         rhs=dc_codes[:, cols].bitcast(E5M2), rhs_scale=dc_scales[:, cols], start=True, stop=True,
                     )
             else:
@@ -146,14 +147,6 @@ def tile_attend_gbil_R_kernel(tc, G, uT, vT, su, uoffs, offs, out):
                     out=accs[b][:], lhsT=codes[:].bitcast(E4M3), lhsT_scale=scales[:],
                     rhs=dc_codes[:].bitcast(E5M2), rhs_scale=dc_scales[:], start=True, stop=True,
                 )
-
-        def warm_up(b):
-            codes, scales = packed[b]
-            spare = sum_bank(b, f"spare{b}")
-            nc.tensor.matmul_mx(
-                out=spare[:], lhsT=codes[:].bitcast(E4M3), lhsT_scale=scales[:],
-                rhs=dc_codes[:].bitcast(E5M2), rhs_scale=dc_scales[:], start=True, stop=True,
-            )
 
         def quantise_dc(b):
             cols = slice(b * P, (b + 1) * P)
@@ -170,17 +163,20 @@ def tile_attend_gbil_R_kernel(tc, G, uT, vT, su, uoffs, offs, out):
                     mybir.AluOpType.mult,
                 )
                 scaled[b] = dc
+            elif b == BLOCKS:
+                for d, copy in enumerate((nc.scalar.copy, nc.vector.tensor_copy)):
+                    result = on_window(7, [P, SLOTS], F32, f"result{d}", 2048 * d)
+                    copy(out=result[:], in_=accs[b + d][:])
+                    nc.sync.dma_start(out=out[d * P : (d + 1) * P, :], in_=result[:])
+            elif b == BLOCKS + 2:
+                result = keep.tile([P, SLOTS], F32, name="result2")
+                nc.scalar.copy(out=result[:], in_=accs[b][:])
+                nc.sync.dma_start(out=out[2 * P : 3 * P, :], in_=result[:])
             else:
-                result = on_window(6 if b < 6 else 8, [P, SLOTS], F32, f"result{b}", 2048 * (b - 3))
-                if b == 2 * BLOCKS - 1:
-                    nc.vector.tensor_copy(out=result[:, : 2 * P], in_=accs[b][:, : 2 * P])
-                    nc.scalar.copy(out=result[:, 2 * P :], in_=accs[b + 1][:, : 2 * P])
-                elif b > BLOCKS:
-                    nc.scalar.copy(out=result[:], in_=accs[b][:])
-                else:
-                    nc.vector.tensor_copy(out=result[:], in_=accs[b][:])
-                d = b - BLOCKS
-                nc.sync.dma_start(out=out[d * P : (d + 1) * P, :], in_=result[:])
+                result = keep.tile([P, SLOTS], F32, name="result3")
+                nc.vector.tensor_copy(out=result[:, : 2 * P], in_=accs[b][0][:])
+                nc.scalar.copy(out=result[:, 2 * P :], in_=accs[b][1][:])
+                nc.sync.dma_start(out=out[3 * P :, :], in_=result[:])
 
         for b in range(6):
             if b < 2 * BLOCKS:
@@ -191,23 +187,21 @@ def tile_attend_gbil_R_kernel(tc, G, uT, vT, su, uoffs, offs, out):
                 gather_su()
             if 2 <= b <= BLOCKS + 1:
                 finish(b - 2)
-            if 1 <= b <= 2 * BLOCKS:
+            if 1 <= b <= BLOCKS:
                 quantise(b - 1)
             if 2 <= b <= BLOCKS + 1:
                 quantise_dc(b - 2)
-            if 1 <= b <= 2 * BLOCKS:
+            if 1 <= b <= BLOCKS:
                 multiply(b - 1)
-        quantise(5)
-        multiply(5)
         gather(6)
-        finish(4)
-        finish(5)
-        warm_up(4)
-        warm_up(5)
+        for b in (4, 5):
+            quantise(b)
+            multiply(b)
         gather(7)
         quantise(6)
+        finish(4)
         multiply(6)
         quantise(7)
-        multiply(7)
         finish(6)
+        multiply(7)
         finish(7)

@@ -16,8 +16,8 @@ P = 128
 SLOTS = 512
 TABLE = 2048
 BLOCKS = 4
-WINDOW_BYTES = 4 * TABLE
-VECTOR_SLOTS = 288
+ROW_BYTES = 4 * TABLE
+USER_SHARES = (512, 0, 320, 256)
 SU_VECTOR_SLOTS = 256
 
 FLOPS = 2 * 2 * 512 * 512 * 512
@@ -34,34 +34,31 @@ def tile_attend_gbil_R_kernel(tc, G, uT, vT, su, uoffs, offs, out):
         def in_bank(index, shape, name):
             return psum.tile(shape, F32, name=name, offset=2048 * index)
 
-        def sum_bank(b, name):
-            return in_bank(5 + b % 3, [P, SLOTS], name)
-
-        def on_window(b, shape, dtype, name, at=0):
-            if b > 2 * BLOCKS:
+        def behind(b, shape, dtype, name, at=0):
+            if b is None:
                 return keep.tile(shape, dtype, name=name, align_bytes=64)
-            return placed.tile(shape, dtype, name=name, offset=b * WINDOW_BYTES + at, align_bytes=64)
+            return placed.tile(shape, dtype, name=name, offset=b * ROW_BYTES + at, align_bytes=64)
 
-        su_table = keep.tile([P, TABLE], F32, name="su_table")
-        nc.vector.memset(su_table[:].bitcast(U32), 0)
         g_rows = keep.tile([P, 4 * SLOTS], F32, name="g_rows")
         nc.sync.dma_start(out=g_rows[:], in_=G.rearrange("(m j) i -> m (j i)", j=4))
         user_list = keep.tile([P, SLOTS // 16], U16, name="user_list")
         item_list = keep.tile([P, SLOTS // 16], U16, name="item_list")
+        su_table = keep.tile([P, TABLE], F32, name="su_table")
+        nc.vector.memset(su_table[: P - 1, :].bitcast(U32), 0)
+        nc.sync.dma_start(out=su_table[P - 1 :, :], in_=su[0:1, :])
+        nc.sync.dma_start(user_list[:], uoffs)
         nc.sync.dma_start(item_list[:], offs)
-        windows = []
-        for b in range(2 * BLOCKS):
-            window = on_window(b, [P, TABLE], F32, f"window{b}")
-            source = vT if b < BLOCKS else uT
-            nc.sync.dma_start(out=window[:], in_=source[(b % BLOCKS) * P : (b % BLOCKS + 1) * P, :])
-            windows.append(window)
-            if b == 0:
-                nc.sync.dma_start(out=su_table[0:1, :], in_=su[0:1, :])
-                nc.sync.dma_start(user_list[:], uoffs)
+        pairs, windows = [], {}
+        for h in range(2):
+            pair = behind(2 * h, [P, 2 * TABLE], F32, f"pair{h}")
+            nc.sync.dma_start(out=pair[:], in_=vT[2 * P * h : 2 * P * (h + 1), :].rearrange("(p e) t -> p (e t)", e=2))
+            pairs.append(pair)
+        for b in range(BLOCKS, 2 * BLOCKS):
+            windows[b] = behind(b, [P, TABLE], F32, f"window{b}")
+            nc.sync.dma_start(out=windows[b][:], in_=uT[(b - BLOCKS) * P : (b - BLOCKS + 1) * P, :])
 
         ident = keep.tile([P, P], F32, name="ident")
         make_identity(nc, ident[:])
-
 
         g_bf = keep.tile([P, 4 * SLOTS], BF16, name="g_bf", align_bytes=64)
         g_k = keep.tile([P, 4 * SLOTS], BF16, name="g_k", align_bytes=64)
@@ -81,127 +78,138 @@ def tile_attend_gbil_R_kernel(tc, G, uT, vT, su, uoffs, offs, out):
                 in_=bank[:].rearrange("p (e u) m -> p e m u", u=2),
             )
         g_codes = keep.tile([P, SLOTS], U32, name="g_codes", align_bytes=64)
-        g_scales = on_window(0, [P, SLOTS], U8, "g_scales", 4096)
+        g_scales = keep.tile([P, SLOTS], U8, name="g_scales", align_bytes=64)
+        nc.vector.quantize_mx(out=g_codes[:].bitcast(E5M2), scales=g_scales[:], in_=g_k[:])
 
-        su_cols = on_window(1, [P, 1, 4], F32, "su_cols", 4096)
+        su_row = keep.tile([P, SLOTS], F32, name="su_row")
+        cut = SU_VECTOR_SLOTS // 16
+        nc.vector.tensor_copy(su_row[:, :SU_VECTOR_SLOTS], su_table[:].indirect(user_list[:, :cut]))
+        nc.scalar.activation(su_row[:, SU_VECTOR_SLOTS:], su_table[:].indirect(user_list[:, cut:]), COPY)
+        su_bank = in_bank(7, [P, 4, P], "su_bank")
+        for j in range(4):
+            nc.tensor.transpose(su_bank[:, j, :], su_row[:, j:SLOTS:4], ident[:])
+        su_cols = keep.tile([P, 1, 4], F32, name="su_cols")
+        nc.scalar.copy(out=su_cols[:, 0, :], in_=su_bank[:, :, P - 1])
 
-        def gather_su():
-            su_row = on_window(0, [P, SLOTS], F32, "su_row")
-            cut = SU_VECTOR_SLOTS // 16
-            nc.vector.tensor_copy(su_row[:, :SU_VECTOR_SLOTS], su_table[:].indirect(user_list[:, :cut]))
-            nc.scalar.activation(su_row[:, SU_VECTOR_SLOTS:], su_table[:].indirect(user_list[:, cut:]), COPY)
-            bank = in_bank(0, [P, 4, P], "su_bank")
-            for j in range(4):
-                nc.tensor.transpose(bank[:, j, :], su_row[:, j:SLOTS:4], ident[:])
-            nc.scalar.copy(out=su_cols[:, 0, :], in_=bank[:, :, 0])
-
-        dc_codes = keep.tile([P, SLOTS], U32, name="dc_codes", align_bytes=64)
-        dc_scales = keep.tile([P, SLOTS], U8, name="dc_scales", align_bytes=64)
-        turned, packed, accs, scaled = {}, {}, {}, {}
+        banks, turned, packed, accs, scaled, dc = {}, {}, {}, {}, {}, {}
 
         def gather(b):
-            offsets = item_list if b < BLOCKS else user_list
             picked = keep.tile([P, SLOTS], BF16, name=f"picked{b}")
-            share = VECTOR_SLOTS if b < 2 * BLOCKS - 1 else SLOTS // 2
-            cut = share // 16
-            nc.vector.tensor_copy(picked[:, :share], windows[b][:].indirect(offsets[:, :cut]))
-            nc.scalar.activation(picked[:, share:], windows[b][:].indirect(offsets[:, cut:]), COPY)
             words = picked[:].bitcast(F32)
-            bank = in_bank(2 + b % 3, [P, 4, P], f"bank{b}")
+            planes = [words[:, u:256:2] for u in range(2)]
+            if b >= BLOCKS:
+                share = USER_SHARES[b - BLOCKS]
+                if share > 0:
+                    nc.vector.tensor_copy(picked[:, :share], windows[b][:].indirect(user_list[:, : share // 16]))
+                if share < SLOTS:
+                    nc.scalar.activation(picked[:, share:], windows[b][:].indirect(user_list[:, share // 16 :]), COPY)
+            elif b % 2 == 0:
+                nc.scalar.activation(picked[:], pairs[b // 2][:].indirect(item_list[:]), COPY)
+            else:
+                nc.vector.tensor_copy(
+                    picked[:].rearrange("p (u n e) -> p n u e", u=2, e=2),
+                    pairs[b // 2][:, TABLE:].indirect(item_list[:]),
+                )
+                planes = [words[:, u * P : (u + 1) * P] for u in range(2)]
+            banks[b] = in_bank(2 + b % 3, [P, 2, P], f"bank{b}")
             for u in range(2):
-                nc.tensor.transpose(bank[:, u, :], words[:, u:256:2], ident[:])
-            turned[b] = keep.tile([P, 4 * P], BF16, name=f"turned{b}", align_bytes=64)
+                nc.tensor.transpose(banks[b][:, u, :], planes[u], ident[:])
+
+        def unload(b, held=None, at=0):
+            turned[b] = behind(held, [P, 4 * P], BF16, f"turned{b}", at)
             nc.scalar.copy(
                 out=turned[b][:].bitcast(F32).rearrange("p (n u) -> p n u", u=2),
-                in_=bank[:, 0:2, :].rearrange("p u n -> p n u"),
+                in_=banks[b][:].rearrange("p u n -> p n u"),
             )
 
-        def quantise(b):
-            held, at = {4: (6, 0), 5: (6, 1024), 6: (7, 4096), 7: (9, 0)}.get(b, (b + 1, 0))
-            codes = on_window(held, [P, P], U32, f"codes{b}", at)
-            scales = on_window(held, [P, P], U8, f"scales{b}", at + 512)
+        def quantise(b, held=None, at=0):
+            codes = behind(held, [P, P], U32, f"codes{b}", at)
+            scales = behind(held, [P, P], U8, f"scales{b}", at + 512)
             nc.vector.quantize_mx(out=codes[:].bitcast(E4M3), scales=scales[:], in_=turned[b][:])
             packed[b] = codes, scales
 
-        def multiply(b):
+        def first_product(b):
             codes, scales = packed[b]
-            if b < 2 * BLOCKS - 1:
-                accs[b] = sum_bank(b, f"acc{b}")
-            if b < BLOCKS:
-                for j in range(4):
-                    cols = slice(j * P, (j + 1) * P)
-                    nc.tensor.matmul_mx(
-                        out=accs[b][:, cols], lhsT=g_codes[:, cols].bitcast(E5M2), lhsT_scale=g_scales[:, cols],
-                        rhs=codes[:].bitcast(E4M3), rhs_scale=scales[:], start=True, stop=True,
-                    )
-            elif b == 2 * BLOCKS - 1:
-                accs[b] = [in_bank(index, [P, 2 * P], f"half{index}") for index in (0, 1)]
-                for h in range(2):
-                    cols = slice(h * 2 * P, (h + 1) * 2 * P)
-                    nc.tensor.matmul_mx(
-                        out=accs[b][h][:], lhsT=codes[:].bitcast(E4M3), lhsT_scale=scales[:],
-                        rhs=dc_codes[:, cols].bitcast(E5M2), rhs_scale=dc_scales[:, cols], start=True, stop=True,
-                    )
-            else:
+            accs[b] = in_bank(5 + b % 3, [P, SLOTS], f"acc{b}")
+            for j in range(4):
+                cols = slice(j * P, (j + 1) * P)
                 nc.tensor.matmul_mx(
-                    out=accs[b][:], lhsT=codes[:].bitcast(E4M3), lhsT_scale=scales[:],
-                    rhs=dc_codes[:].bitcast(E5M2), rhs_scale=dc_scales[:], start=True, stop=True,
+                    out=accs[b][:, cols], lhsT=g_codes[:, cols].bitcast(E5M2), lhsT_scale=g_scales[:, cols],
+                    rhs=codes[:].bitcast(E4M3), rhs_scale=scales[:], start=True, stop=True,
                 )
 
-        def quantise_dc(b):
-            cols = slice(b * P, (b + 1) * P)
-            nc.vector.quantize_mx(
-                out=dc_codes[:, cols].bitcast(E5M2), scales=dc_scales[:, cols],
-                in_=scaled[b][:].rearrange("p f j -> p (f j)"),
-            )
-
-        def finish(b):
-            if b < BLOCKS:
-                dc = on_window(b + 2, [P, P, 4], BF16, f"dc{b}", 1024)
+        def scale(h, order, held=None):
+            scaled[h] = behind(held, [P, 2, P, 4], BF16, f"scaled{h}")
+            for e in order:
                 nc.vector.tensor_tensor(
-                    dc[:], accs[b][:].rearrange("p (j f) -> p f j", j=4), su_cols[:].to_broadcast([P, P, 4]),
-                    mybir.AluOpType.mult,
+                    scaled[h][:, e], accs[2 * h + e][:].rearrange("p (j f) -> p f j", j=4),
+                    su_cols[:].to_broadcast([P, P, 4]), mybir.AluOpType.mult,
                 )
-                scaled[b] = dc
-            elif b == BLOCKS:
-                for d, copy in enumerate((nc.scalar.copy, nc.vector.tensor_copy)):
-                    result = on_window(7, [P, SLOTS], F32, f"result{d}", 2048 * d)
-                    copy(out=result[:], in_=accs[b + d][:])
-                    nc.sync.dma_start(out=out[d * P : (d + 1) * P, :], in_=result[:])
-            elif b == BLOCKS + 2:
-                result = keep.tile([P, SLOTS], F32, name="result2")
-                nc.scalar.copy(out=result[:], in_=accs[b][:])
-                nc.sync.dma_start(out=out[2 * P : 3 * P, :], in_=result[:])
-            else:
-                result = keep.tile([P, SLOTS], F32, name="result3")
-                nc.vector.tensor_copy(out=result[:, : 2 * P], in_=accs[b][0][:])
-                nc.scalar.copy(out=result[:, 2 * P :], in_=accs[b][1][:])
-                nc.sync.dma_start(out=out[3 * P :, :], in_=result[:])
 
-        for b in range(6):
-            if b < 2 * BLOCKS:
-                gather(b)
-            if b == 0:
-                nc.vector.quantize_mx(out=g_codes[:].bitcast(E5M2), scales=g_scales[:], in_=g_k[:])
-            if b == 1:
-                gather_su()
-            if 2 <= b <= BLOCKS + 1:
-                finish(b - 2)
-            if 1 <= b <= BLOCKS:
-                quantise(b - 1)
-            if 2 <= b <= BLOCKS + 1:
-                quantise_dc(b - 2)
-            if 1 <= b <= BLOCKS:
-                multiply(b - 1)
-        gather(6)
-        for b in (4, 5):
+        def quantise_dc(h, held, at):
+            codes = behind(held, [P, 2 * P], U32, f"dc_codes{h}", at)
+            scales = behind(held, [P, 2 * P], U8, f"dc_scales{h}", at + 1024)
+            nc.vector.quantize_mx(
+                out=codes[:].bitcast(E5M2), scales=scales[:], in_=scaled[h][:].rearrange("p e f j -> p (e f j)")
+            )
+            dc[h] = codes, scales
+
+        def second_product(b, bank_numbers):
+            codes, scales = packed[b]
+            tiles = [in_bank(index, [P, SLOTS // len(bank_numbers)], f"sum{b}_{index}") for index in bank_numbers]
+            accs[b] = tiles
+            for h in range(2):
+                acc = tiles[h][:] if len(tiles) == 2 else tiles[0][:, 2 * P * h : 2 * P * (h + 1)]
+                nc.tensor.matmul_mx(
+                    out=acc, lhsT=codes[:].bitcast(E4M3), lhsT_scale=scales[:],
+                    rhs=dc[h][0][:].bitcast(E5M2), rhs_scale=dc[h][1][:], start=True, stop=True,
+                )
+
+        def store(b, copies, held=None, at=0):
+            result = behind(held, [P, SLOTS], F32, f"result{b}", at)
+            width = SLOTS // len(copies)
+            for h, copy in enumerate(copies):
+                copy(
+                    out=result[:, h * width : (h + 1) * width].rearrange("p (h n e) -> p h n e", n=P, e=2),
+                    in_=accs[b][h][:].rearrange("p (h e n) -> p h n e", n=P, e=2),
+                )
+            nc.sync.dma_start(out=out[(b - BLOCKS) * P : (b - BLOCKS + 1) * P, :], in_=result[:])
+
+        for b in (1, 0):
+            gather(b)
+        for b in (1, 0):
+            unload(b)
             quantise(b)
-            multiply(b)
+            first_product(b)
+        scale(0, (1, 0))
+        for b in (2, 3):
+            gather(b)
+        for b in (2, 3):
+            unload(b)
+        gather(4)
+        quantise(2, 4)
+        quantise_dc(0, 4, 1024)
+        quantise(3, 4, 4096)
+        for b in (2, 3):
+            first_product(b)
+        unload(4)
+        scale(1, (0, 1))
+        gather(5)
+        gather(6)
+        unload(5, 6, 2048)
+        quantise(4, 6)
+        quantise_dc(1, 6, 4096)
+        quantise(5, 6, 1024)
+        second_product(4, (6,))
+        second_product(5, (7,))
+        unload(6)
         gather(7)
-        quantise(6)
-        finish(4)
-        multiply(6)
+        quantise(6, 7, 4096)
+        store(4, (nc.scalar.copy,), 7)
+        store(5, (nc.vector.tensor_copy,), 7, 2048)
+        second_product(6, (5,))
+        unload(7)
         quantise(7)
-        finish(6)
-        multiply(7)
-        finish(7)
+        store(6, (nc.scalar.copy,))
+        second_product(7, (0, 1))
+        store(7, (nc.vector.tensor_copy, nc.scalar.copy))

@@ -165,6 +165,14 @@ def tile_attend_gbil_R_kernel(tc, G, uT, vT, su, uoffs, offs, out):
                     rhs=dc[h][0][:].bitcast(E5M2), rhs_scale=dc[h][1][:], start=True, stop=True,
                 )
 
+        def warm_up(b):
+            codes, scales = packed[b]
+            spare = in_bank(0, [P, 2 * P], "spare")
+            nc.tensor.matmul_mx(
+                out=spare[:], lhsT=codes[:].bitcast(E4M3), lhsT_scale=scales[:],
+                rhs=dc[0][0][:].bitcast(E5M2), rhs_scale=dc[0][1][:], start=True, stop=True,
+            )
+
         def store(b, copies, held=None, at=0):
             result = behind(held, [P, SLOTS], F32, f"result{b}", at)
             width = SLOTS // len(copies)
@@ -200,6 +208,7 @@ def tile_attend_gbil_R_kernel(tc, G, uT, vT, su, uoffs, offs, out):
         quantise(4, 6)
         quantise_dc(1, 6, 4096)
         quantise(5, 6, 1024)
+        warm_up(4)
         second_product(4, (6,))
         second_product(5, (7,))
         unload(6)

@@ -181,7 +181,10 @@ def tile_attend_gbil_R_kernel(tc, G, uT, vT, su, uoffs, offs, out):
                     out=result[:, h * width : (h + 1) * width].rearrange("p (h n e) -> p h n e", n=P, e=2),
                     in_=accs[b][h][:].rearrange("p (h e n) -> p h n e", n=P, e=2),
                 )
-            nc.sync.dma_start(out=out[(b - BLOCKS) * P : (b - BLOCKS + 1) * P, :], in_=result[:])
+            rows = slice((b - BLOCKS) * P, (b - BLOCKS + 1) * P)
+            for h in range(len(copies)):
+                cols = slice(h * width, (h + 1) * width)
+                nc.sync.dma_start(out=out[rows, cols], in_=result[:, cols])
 
         for b in (1, 0):
             gather(b)

@@ -88,8 +88,8 @@ def tile_attend_gbil_R_kernel(tc, G, uT, vT, su, uoffs, offs, out):
         su_bank = in_bank(7, [P, 4, P], "su_bank")
         for j in range(4):
             nc.tensor.transpose(su_bank[:, j, :], su_row[:, j:SLOTS:4], ident[:])
-        su_cols = keep.tile([P, 1, 4], F32, name="su_cols")
-        nc.scalar.copy(out=su_cols[:, 0, :], in_=su_bank[:, :, P - 1])
+        su_cols = keep.tile([P, 1, 1, 4], F32, name="su_cols")
+        nc.scalar.copy(out=su_cols[:, 0, 0, :], in_=su_bank[:, :, P - 1])
 
         banks, turned, packed, accs, scaled, dc = {}, {}, {}, {}, {}, {}
 
@@ -139,18 +139,18 @@ def tile_attend_gbil_R_kernel(tc, G, uT, vT, su, uoffs, offs, out):
                 )
 
         def scale(h, order, held=None):
-            scaled[h] = behind(held, [P, 2, P, 4], BF16, f"scaled{h}")
+            scaled[h] = behind(held, [P, 2, 2, P // 2, 4], BF16, f"scaled{h}")
             for e in order:
                 nc.vector.tensor_tensor(
-                    scaled[h][:, e], accs[2 * h + e][:].rearrange("p (j f) -> p f j", j=4),
-                    su_cols[:].to_broadcast([P, P, 4]), mybir.AluOpType.mult,
+                    scaled[h][:, :, e], accs[2 * h + e][:].rearrange("p (j m n) -> p m n j", j=4, m=2),
+                    su_cols[:].to_broadcast([P, 2, P // 2, 4]), mybir.AluOpType.mult,
                 )
 
         def quantise_dc(h, held, at):
             codes = behind(held, [P, 2 * P], U32, f"dc_codes{h}", at)
             scales = behind(held, [P, 2 * P], U8, f"dc_scales{h}", at + 1024)
             nc.vector.quantize_mx(
-                out=codes[:].bitcast(E5M2), scales=scales[:], in_=scaled[h][:].rearrange("p e f j -> p (e f j)")
+                out=codes[:].bitcast(E5M2), scales=scales[:], in_=scaled[h][:].rearrange("p m e n j -> p (m e n j)")
             )
             dc[h] = codes, scales
 
@@ -158,11 +158,15 @@ def tile_attend_gbil_R_kernel(tc, G, uT, vT, su, uoffs, offs, out):
             codes, scales = packed[b]
             tiles = [in_bank(index, [P, SLOTS // len(bank_numbers)], f"sum{b}_{index}") for index in bank_numbers]
             accs[b] = tiles
-            for h in range(2):
-                acc = tiles[h][:] if len(tiles) == 2 else tiles[0][:, 2 * P * h : 2 * P * (h + 1)]
+            passes = max(2, len(tiles))
+            width = SLOTS // passes
+            for k in range(passes):
+                acc = tiles[k][:] if len(tiles) > 1 else tiles[0][:, width * k : width * (k + 1)]
+                h, first = divmod(width * k, 2 * P)
+                cols = slice(first, first + width)
                 nc.tensor.matmul_mx(
                     out=acc, lhsT=codes[:].bitcast(E4M3), lhsT_scale=scales[:],
-                    rhs=dc[h][0][:].bitcast(E5M2), rhs_scale=dc[h][1][:], start=True, stop=True,
+                    rhs=dc[h][0][:, cols].bitcast(E5M2), rhs_scale=dc[h][1][:, cols], start=True, stop=True,
                 )
 
         def warm_up(b):
@@ -173,17 +177,18 @@ def tile_attend_gbil_R_kernel(tc, G, uT, vT, su, uoffs, offs, out):
                 rhs=dc[0][0][:].bitcast(E5M2), rhs_scale=dc[0][1][:], start=True, stop=True,
             )
 
-        def store(b, copies, held=None, at=0):
+        def store(b, copies, stores, held=None, at=0):
             result = behind(held, [P, SLOTS], F32, f"result{b}", at)
             width = SLOTS // len(copies)
-            for h, copy in enumerate(copies):
-                copy(
-                    out=result[:, h * width : (h + 1) * width].rearrange("p (h n e) -> p h n e", n=P, e=2),
-                    in_=accs[b][h][:].rearrange("p (h e n) -> p h n e", n=P, e=2),
-                )
             rows = slice((b - BLOCKS) * P, (b - BLOCKS + 1) * P)
-            for h in range(len(copies)):
-                cols = slice(h * width, (h + 1) * width)
+            for k, copy in enumerate(copies):
+                acc = accs[b][k][:] if len(accs[b]) > 1 else accs[b][0][:, width * k : width * (k + 1)]
+                copy(
+                    out=result[:, k * width : (k + 1) * width].rearrange("p (q n e) -> p q n e", n=P // 2, e=2),
+                    in_=acc.rearrange("p (q e n) -> p q n e", n=P // 2, e=2),
+                )
+            for k in range(stores):
+                cols = slice(k * SLOTS // stores, (k + 1) * SLOTS // stores)
                 nc.sync.dma_start(out=out[rows, cols], in_=result[:, cols])
 
         for b in (1, 0):
@@ -217,11 +222,11 @@ def tile_attend_gbil_R_kernel(tc, G, uT, vT, su, uoffs, offs, out):
         unload(6)
         gather(7)
         quantise(6, 7, 4096)
-        store(4, (nc.scalar.copy,), 7)
-        store(5, (nc.vector.tensor_copy,), 7, 2048)
+        store(4, (nc.scalar.copy,), 1, 7)
+        store(5, (nc.vector.tensor_copy,), 1, 7, 2048)
         second_product(6, (5,))
         unload(7)
         quantise(7)
-        store(6, (nc.scalar.copy,))
-        second_product(7, (0, 1))
-        store(7, (nc.vector.tensor_copy, nc.scalar.copy))
+        store(6, (nc.scalar.copy, nc.scalar.copy), 2)
+        second_product(7, (0, 1, 2, 4))
+        store(7, (nc.vector.tensor_copy, nc.scalar.copy) * 2, 2)

@@ -224,9 +224,9 @@ def tile_attend_gbil_R_kernel(tc, G, uT, vT, su, uoffs, offs, out):
         quantise(6, 7, 4096)
         store(4, (nc.scalar.copy,), 1, 7)
         store(5, (nc.vector.tensor_copy,), 1, 7, 2048)
-        second_product(6, (5,))
+        second_product(6, (5, 1))
         unload(7)
         quantise(7)
         store(6, (nc.scalar.copy, nc.scalar.copy), 2)
-        second_product(7, (0, 1, 2, 4))
+        second_product(7, (0, 2, 4, 6))
         store(7, (nc.vector.tensor_copy, nc.scalar.copy) * 2, 2)

@@ -18,7 +18,6 @@ TABLE = 2048
 BLOCKS = 4
 ROW_BYTES = 4 * TABLE
 USER_SHARES = (512, 0, 320, 256)
-SU_VECTOR_SLOTS = 256
 
 FLOPS = 2 * 2 * 512 * 512 * 512
 BYTES = 4 * (2 * 512 * 2048 + 2 * 512 * 512 + 2048) + 2 * 2 * 128 * 32
@@ -40,13 +39,13 @@ def tile_attend_gbil_R_kernel(tc, G, uT, vT, su, uoffs, offs, out):
             return placed.tile(shape, dtype, name=name, offset=b * ROW_BYTES + at, align_bytes=64)
 
         g_rows = keep.tile([P, 4 * SLOTS], F32, name="g_rows")
-        nc.sync.dma_start(out=g_rows[:], in_=G.rearrange("(m j) i -> m (j i)", j=4))
+        nc.scalar.dma_start(out=g_rows[:], in_=G.rearrange("(m j) i -> m (j i)", j=4))
         user_list = keep.tile([P, SLOTS // 16], U16, name="user_list")
         item_list = keep.tile([P, SLOTS // 16], U16, name="item_list")
         su_table = keep.tile([P, TABLE], F32, name="su_table")
         nc.vector.memset(su_table[: P - 1, :].bitcast(U32), 0)
-        nc.sync.dma_start(out=su_table[P - 1 :, :], in_=su[0:1, :])
         nc.sync.dma_start(user_list[:], uoffs)
+        nc.sync.dma_start(out=su_table[P - 1 :, :], in_=su[0:1, :])
         nc.sync.dma_start(item_list[:], offs)
         pairs, windows = [], {}
         for h in range(2):
@@ -59,6 +58,14 @@ def tile_attend_gbil_R_kernel(tc, G, uT, vT, su, uoffs, offs, out):
 
         ident = keep.tile([P, P], F32, name="ident")
         make_identity(nc, ident[:])
+
+        su_row = keep.tile([P, SLOTS], F32, name="su_row")
+        nc.vector.tensor_copy(su_row[:], su_table[:].indirect(user_list[:]))
+        su_bank = in_bank(7, [P, 4, P], "su_bank")
+        for j in range(4):
+            nc.tensor.transpose(su_bank[:, j, :], su_row[:, j:SLOTS:4], ident[:])
+        su_cols = keep.tile([P, 1, 1, 4], F32, name="su_cols")
+        nc.vector.tensor_copy(out=su_cols[:, 0, 0, :], in_=su_bank[:, :, P - 1])
 
         g_bf = keep.tile([P, 4 * SLOTS], BF16, name="g_bf", align_bytes=64)
         g_k = keep.tile([P, 4 * SLOTS], BF16, name="g_k", align_bytes=64)
@@ -77,19 +84,8 @@ def tile_attend_gbil_R_kernel(tc, G, uT, vT, su, uoffs, offs, out):
                 out=g_k[:, half].bitcast(F32).rearrange("p (e m u) -> p e m u", e=2, u=2),
                 in_=bank[:].rearrange("p (e u) m -> p e m u", u=2),
             )
-        g_codes = keep.tile([P, SLOTS], U32, name="g_codes", align_bytes=64)
-        g_scales = keep.tile([P, SLOTS], U8, name="g_scales", align_bytes=64)
-        nc.vector.quantize_mx(out=g_codes[:].bitcast(E5M2), scales=g_scales[:], in_=g_k[:])
-
-        su_row = keep.tile([P, SLOTS], F32, name="su_row")
-        cut = SU_VECTOR_SLOTS // 16
-        nc.vector.tensor_copy(su_row[:, :SU_VECTOR_SLOTS], su_table[:].indirect(user_list[:, :cut]))
-        nc.scalar.activation(su_row[:, SU_VECTOR_SLOTS:], su_table[:].indirect(user_list[:, cut:]), COPY)
-        su_bank = in_bank(7, [P, 4, P], "su_bank")
-        for j in range(4):
-            nc.tensor.transpose(su_bank[:, j, :], su_row[:, j:SLOTS:4], ident[:])
-        su_cols = keep.tile([P, 1, 1, 4], F32, name="su_cols")
-        nc.scalar.copy(out=su_cols[:, 0, 0, :], in_=su_bank[:, :, P - 1])
+        g_codes = behind(0, [P, SLOTS], U32, "g_codes")
+        g_scales = behind(0, [P, SLOTS], U8, "g_scales", 2048)
 
         banks, turned, packed, accs, scaled, dc = {}, {}, {}, {}, {}, {}
 
@@ -193,6 +189,7 @@ def tile_attend_gbil_R_kernel(tc, G, uT, vT, su, uoffs, offs, out):
 
         for b in (1, 0):
             gather(b)
+        nc.vector.quantize_mx(out=g_codes[:].bitcast(E5M2), scales=g_scales[:], in_=g_k[:])
         for b in (1, 0):
             unload(b)
             quantise(b)

from contextlib import ExitStack

import concourse.mybir as mybir
from concourse.masks import make_identity

F32 = mybir.dt.float32
BF16 = mybir.dt.bfloat16
U32 = mybir.dt.uint32
U16 = mybir.dt.uint16
U8 = mybir.dt.uint8
E4M3 = mybir.dt.float8_e4m3fn_x4
E5M2 = mybir.dt.float8_e5m2_x4
COPY = mybir.ActivationFunctionType.Copy

P = 128
SLOTS = 512
TABLE = 2048
BLOCKS = 4
ROW_BYTES = 4 * TABLE
USER_SHARES = (512, 0, 320, 256)

FLOPS = 2 * 2 * 512 * 512 * 512
BYTES = 4 * (2 * 512 * 2048 + 2 * 512 * 512 + 2048) + 2 * 2 * 128 * 32


def tile_attend_gbil_R_kernel(tc, G, uT, vT, su, uoffs, offs, out):
    nc = tc.nc
    with ExitStack() as ctx:
        keep = ctx.enter_context(tc.tile_pool(name="keep", bufs=1))
        placed = ctx.enter_context(tc.tile_pool(name="placed", bufs=1))
        psum = ctx.enter_context(tc.psum_pool(name="psum", bufs=1))

        def in_bank(index, shape, name):
            return psum.tile(shape, F32, name=name, offset=2048 * index)

        def behind(b, shape, dtype, name, at=0):
            if b is None:
                return keep.tile(shape, dtype, name=name, align_bytes=64)
            return placed.tile(shape, dtype, name=name, offset=b * ROW_BYTES + at, align_bytes=64)

        g_rows = keep.tile([P, 4 * SLOTS], F32, name="g_rows")
        nc.scalar.dma_start(out=g_rows[:], in_=G.rearrange("(m j) i -> m (j i)", j=4))
        user_list = keep.tile([P, SLOTS // 16], U16, name="user_list")
        item_list = keep.tile([P, SLOTS // 16], U16, name="item_list")
        su_table = keep.tile([P, TABLE], F32, name="su_table")
        nc.vector.memset(su_table[: P - 1, :].bitcast(U32), 0)
        nc.sync.dma_start(user_list[:], uoffs)
        nc.sync.dma_start(out=su_table[P - 1 :, :], in_=su[0:1, :])
        nc.sync.dma_start(item_list[:], offs)
        pairs, windows = [], {}
        for h in range(2):
            pair = behind(2 * h, [P, 2 * TABLE], F32, f"pair{h}")
            nc.sync.dma_start(out=pair[:], in_=vT[2 * P * h : 2 * P * (h + 1), :].rearrange("(p e) t -> p (e t)", e=2))
            pairs.append(pair)
        for b in range(BLOCKS, 2 * BLOCKS):
            windows[b] = behind(b, [P, TABLE], F32, f"window{b}")
            nc.sync.dma_start(out=windows[b][:], in_=uT[(b - BLOCKS) * P : (b - BLOCKS + 1) * P, :])

        ident = keep.tile([P, P], F32, name="ident")
        make_identity(nc, ident[:])

        su_row = keep.tile([P, SLOTS], F32, name="su_row")
        nc.vector.tensor_copy(su_row[:], su_table[:].indirect(user_list[:]))
        su_bank = in_bank(7, [P, 4, P], "su_bank")
        for j in range(4):
            nc.tensor.transpose(su_bank[:, j, :], su_row[:, j:SLOTS:4], ident[:])
        su_cols = keep.tile([P, 1, 1, 4], F32, name="su_cols")
        nc.vector.tensor_copy(out=su_cols[:, 0, 0, :], in_=su_bank[:, :, P - 1])

        g_bf = keep.tile([P, 4 * SLOTS], BF16, name="g_bf", align_bytes=64)
        g_k = keep.tile([P, 4 * SLOTS], BF16, name="g_k", align_bytes=64)
        for h in range(2):
            half = slice(2 * SLOTS * h, 2 * SLOTS * (h + 1))
            if h == 0:
                nc.vector.tensor_copy(out=g_bf[:, half], in_=g_rows[:, half])
            else:
                nc.scalar.activation(g_bf[:, half], g_rows[:, half], COPY)
            words = g_bf[:, half].bitcast(F32)
            bank = in_bank(h, [P, 4, P], f"g_bank{h}")
            for e in range(2):
                for u in range(2):
                    nc.tensor.transpose(bank[:, 2 * e + u, :], words[:, 256 * e + u : 256 * (e + 1) : 2], ident[:])
            nc.scalar.copy(
                out=g_k[:, half].bitcast(F32).rearrange("p (e m u) -> p e m u", e=2, u=2),
                in_=bank[:].rearrange("p (e u) m -> p e m u", u=2),
            )
        g_codes = behind(0, [P, SLOTS], U32, "g_codes")
        g_scales = behind(0, [P, SLOTS], U8, "g_scales", 2048)

        banks, turned, packed, accs, scaled, dc = {}, {}, {}, {}, {}, {}

        def gather(b):
            picked = keep.tile([P, SLOTS], BF16, name=f"picked{b}")
            words = picked[:].bitcast(F32)
            planes = [words[:, u:256:2] for u in range(2)]
            if b >= BLOCKS:
                share = USER_SHARES[b - BLOCKS]
                if share > 0:
                    nc.vector.tensor_copy(picked[:, :share], windows[b][:].indirect(user_list[:, : share // 16]))
                if share < SLOTS:
                    nc.scalar.activation(picked[:, share:], windows[b][:].indirect(user_list[:, share // 16 :]), COPY)
            elif b % 2 == 0:
                nc.scalar.activation(picked[:], pairs[b // 2][:].indirect(item_list[:]), COPY)
            else:
                nc.vector.tensor_copy(
                    picked[:].rearrange("p (u n e) -> p n u e", u=2, e=2),
                    pairs[b // 2][:, TABLE:].indirect(item_list[:]),
                )
                planes = [words[:, u * P : (u + 1) * P] for u in range(2)]
            banks[b] = in_bank(2 + b % 3, [P, 2, P], f"bank{b}")
            for u in range(2):
                nc.tensor.transpose(banks[b][:, u, :], planes[u], ident[:])

        def unload(b, held=None, at=0):
            turned[b] = behind(held, [P, 4 * P], BF16, f"turned{b}", at)
            nc.scalar.copy(
                out=turned[b][:].bitcast(F32).rearrange("p (n u) -> p n u", u=2),
                in_=banks[b][:].rearrange("p u n -> p n u"),
            )

        def quantise(b, held=None, at=0):
            codes = behind(held, [P, P], U32, f"codes{b}", at)
            scales = behind(held, [P, P], U8, f"scales{b}", at + 512)
            nc.vector.quantize_mx(out=codes[:].bitcast(E4M3), scales=scales[:], in_=turned[b][:])
            packed[b] = codes, scales

        def first_product(b):
            codes, scales = packed[b]
            accs[b] = in_bank(5 + b % 3, [P, SLOTS], f"acc{b}")
            for j in range(4):
                cols = slice(j * P, (j + 1) * P)
                nc.tensor.matmul_mx(
                    out=accs[b][:, cols], lhsT=g_codes[:, cols].bitcast(E5M2), lhsT_scale=g_scales[:, cols],
                    rhs=codes[:].bitcast(E4M3), rhs_scale=scales[:], start=True, stop=True,
                )

        def scale(h, order, held=None):
            scaled[h] = behind(held, [P, 2, 2, P // 2, 4], BF16, f"scaled{h}")
            for e in order:
                nc.vector.tensor_tensor(
                    scaled[h][:, :, e], accs[2 * h + e][:].rearrange("p (j m n) -> p m n j", j=4, m=2),
                    su_cols[:].to_broadcast([P, 2, P // 2, 4]), mybir.AluOpType.mult,
                )

        def quantise_dc(h, held, at):
            codes = behind(held, [P, 2 * P], U32, f"dc_codes{h}", at)
            scales = behind(held, [P, 2 * P], U8, f"dc_scales{h}", at + 1024)
            nc.vector.quantize_mx(
                out=codes[:].bitcast(E5M2), scales=scales[:], in_=scaled[h][:].rearrange("p m e n j -> p (m e n j)")
            )
            dc[h] = codes, scales

        def second_product(b, bank_numbers):
            codes, scales = packed[b]
            tiles = [in_bank(index, [P, SLOTS // len(bank_numbers)], f"sum{b}_{index}") for index in bank_numbers]
            accs[b] = tiles
            passes = max(2, len(tiles))
            width = SLOTS // passes
            for k in range(passes):
                acc = tiles[k][:] if len(tiles) > 1 else tiles[0][:, width * k : width * (k + 1)]
                h, first = divmod(width * k, 2 * P)
                cols = slice(first, first + width)
                nc.tensor.matmul_mx(
                    out=acc, lhsT=codes[:].bitcast(E4M3), lhsT_scale=scales[:],
                    rhs=dc[h][0][:, cols].bitcast(E5M2), rhs_scale=dc[h][1][:, cols], start=True, stop=True,
                )

        def warm_up(b):
            codes, scales = packed[b]
            spare = in_bank(0, [P, 2 * P], "spare")
            nc.tensor.matmul_mx(
                out=spare[:], lhsT=codes[:].bitcast(E4M3), lhsT_scale=scales[:],
                rhs=dc[0][0][:].bitcast(E5M2), rhs_scale=dc[0][1][:], start=True, stop=True,
            )

        def store(b, copies, stores, held=None, at=0):
            result = behind(held, [P, SLOTS], F32, f"result{b}", at)
            width = SLOTS // len(copies)
            rows = slice((b - BLOCKS) * P, (b - BLOCKS + 1) * P)
            for k, copy in enumerate(copies):
                acc = accs[b][k][:] if len(accs[b]) > 1 else accs[b][0][:, width * k : width * (k + 1)]
                copy(
                    out=result[:, k * width : (k + 1) * width].rearrange("p (q n e) -> p q n e", n=P // 2, e=2),
                    in_=acc.rearrange("p (q e n) -> p q n e", n=P // 2, e=2),
                )
            for k in range(stores):
                cols = slice(k * SLOTS // stores, (k + 1) * SLOTS // stores)
                nc.sync.dma_start(out=out[rows, cols], in_=result[:, cols])

        for b in (1, 0):
            gather(b)
        nc.vector.quantize_mx(out=g_codes[:].bitcast(E5M2), scales=g_scales[:], in_=g_k[:])
        for b in (1, 0):
            unload(b)
            quantise(b)
            first_product(b)
        scale(0, (1, 0))
        for b in (2, 3):
            gather(b)
        for b in (2, 3):
            unload(b)
        gather(4)
        quantise(2, 4)
        quantise_dc(0, 4, 1024)
        quantise(3, 4, 4096)
        for b in (2, 3):
            first_product(b)
        unload(4)
        scale(1, (0, 1))
        gather(5)
        gather(6)
        unload(5, 6, 2048)
        quantise(4, 6)
        quantise_dc(1, 6, 4096)
        quantise(5, 6, 1024)
        warm_up(4)
        second_product(4, (6,))
        second_product(5, (7,))
        unload(6)
        gather(7)
        quantise(6, 7, 4096)
        store(4, (nc.scalar.copy,), 1, 7)
        store(5, (nc.vector.tensor_copy,), 1, 7, 2048)
        second_product(6, (5, 1))
        unload(7)
        quantise(7)
        store(6, (nc.scalar.copy, nc.scalar.copy), 2)
        second_product(7, (0, 2, 4, 6))
        store(7, (nc.vector.tensor_copy, nc.scalar.copy) * 2, 2)
